import numpy as np
import ml_dtypes


def mxq(x, axis, fmt="e4m3"):
    dtype, down = {"e4m3": (ml_dtypes.float8_e4m3fn, 7), "e5m2": (ml_dtypes.float8_e5m2, 14)}[fmt]
    v = np.moveaxis(np.asarray(x, np.float32).astype(ml_dtypes.bfloat16).astype(np.float64), axis, -1)
    blocks = v.reshape(v.shape[:-1] + (-1, 32))
    amax = np.abs(blocks).max(-1, keepdims=True)
    byte = np.maximum(np.where(amax > 0, np.frexp(amax)[1] - 1 + 127, 0) - down, 1)
    scale = np.exp2(byte - 127.0)
    codes = (blocks / scale).astype(np.float32).astype(dtype).astype(np.float64)
    return np.moveaxis((codes * scale).reshape(v.shape), -1, axis)


WIDE = False


def mx_kscale(k):
    if not WIDE:
        return np.ones(k)
    levels = np.array([10, -10, 5, -5, 0])
    if k % 512:
        return np.exp2(np.random.permutation(np.resize(levels, k // 32))).repeat(32)
    a = np.empty((k // 512, 16))
    for p in range(k // 512):
        a[p, :8] = np.random.permutation(np.resize(levels, 8))
        for g in range(8):
            far = levels[np.abs(levels - a[p, g]) >= 10]
            a[p, g + 8] = far[np.random.randint(len(far))]
    return np.exp2(a.ravel()).repeat(32)


def f64(x):
    return np.asarray(x).astype(np.float64)


def striped(idx):
    return np.tile(idx.reshape(-1, 16).T, (8, 1)).astype(np.uint16)


def unstriped(offs):
    return offs[:16].T.reshape(-1).astype(np.int64)


def pack_weight(w):
    k, n = w.shape
    w = f64(np.asarray(w, np.float32).astype(ml_dtypes.bfloat16)).reshape(k // 32, 32, n)
    amax = np.abs(w).max(1)
    byte = np.clip(np.where(amax > 0, np.frexp(amax)[1] - 1 + 127 - 7, 1), 1, 254)
    scaled = (w * np.exp2(127.0 - byte)[:, None, :]).reshape(k, n).astype(np.float32)
    words = np.ascontiguousarray(scaled.reshape(k // 512, 128, 4, n).transpose(0, 1, 3, 2)).astype(ml_dtypes.float8_e4m3fn).view(np.uint8)
    return words, np.ascontiguousarray(byte.astype(np.uint8).reshape(k // 512, 16, n))


def unpack_weight(words, scales):
    g, p, n, _ = words.shape
    vals = np.ascontiguousarray(words).view(ml_dtypes.float8_e4m3fn).astype(np.float64) * np.repeat(np.exp2(scales.astype(np.float64) - 127.0), 8, axis=1)[..., None]
    return vals.transpose(0, 1, 3, 2).reshape(g * 512, n)


def planes(y):
    n, m = y.shape
    v = y.astype(np.float32).astype(ml_dtypes.bfloat16).astype(np.float64).reshape(n // 32, 32, m)
    top = np.abs(v).max(1)
    byte = np.clip(np.where(top > 0, np.frexp(top)[1] - 1 + 127 - 7, 1), 1, 254)
    codes = (v * np.exp2(127.0 - byte)[:, None, :]).reshape(n, m).astype(np.float32).astype(ml_dtypes.float8_e4m3fn).view(np.uint8)
    words = codes.reshape(n // 512, 128, 4, m).transpose(0, 1, 3, 2)
    return np.ascontiguousarray(words), np.ascontiguousarray(byte.astype(np.uint8).reshape(n // 512, 16, m))


def gelu(v):
    return 0.5 * v * (1.0 + np.tanh(np.sqrt(2.0 / np.pi) * (v + 0.044715 * v**3)))


K, T, S, D, V, H, N, U = 1024, 2048, 1024, 2, 512, 512, 512, 256
P = 2 ** 7


def setup_inputs():
    n = np.random.standard_normal
    s = mx_kscale(K)[:, None]
    u = mx_kscale(H)
    near = np.random.permutation(S)
    next_ = np.random.permutation(V)
    packed_xT = pack_weight(n((K, T)) * s)
    return {
        "x_words": packed_xT[0],
        "x_scales": packed_xT[1],
        "w1": (n((K, H)) / np.sqrt(K) / s * u).astype(np.float32),
        "w2": (n((H, N)) / np.sqrt(H) / u[:, None]).astype(np.float32),
        "gate": (np.tile(np.random.uniform(0.2, 1.0, (D, 1, V)) / np.sqrt(D), (1, P, 1))).astype(np.float32),
        "gate2": (np.tile(np.random.uniform(0.2, 1.0, (D, 1, U)) / np.sqrt(D), (1, P, 1))).astype(np.float32),
        "offs": striped(np.random.permutation(T)[:S]),
        "cen": striped(np.random.permutation(S)[:V]),
        "pos1": striped(near[:V]),
        "pos2": striped(near[V:]),
        "nxt1": striped(next_[:U]),
        "nxt2": striped(next_[U:]),
        "root": striped(np.random.permutation(S)[:U]),
    }


def reference(x_words, x_scales, w1, w2, gate, gate2, offs, cen, pos1, pos2, nxt1, nxt2, root):
    xq = unpack_weight(x_words, x_scales)[:, unstriped(offs)]
    h = gelu(mxq(f64(w1), 0, "e4m3").T @ xq)
    y = mxq(f64(w2), 0, "e4m3").T @ mxq(h, 0, "e4m3")
    z = 0.8 * (y[:, unstriped(pos1)] * f64(gate)[0, :1] + y[:, unstriped(pos2)] * f64(gate)[1, :1]) + 0.2 * y[:, unstriped(cen)]
    out_0 = 0.8 * (z[:, unstriped(nxt1)] * f64(gate2)[0, :1] + z[:, unstriped(nxt2)] * f64(gate2)[1, :1]) + 0.2 * y[:, unstriped(root)]
    return (out_0,) + planes(out_0)

@@ -1,0 +1,248 @@
+from contextlib import ExitStack
+
+import concourse.mybir as mybir
+from concourse.masks import make_identity
+
+K, T, S, V, H, N, U = 1024, 2048, 1024, 512, 512, 512, 256
+FLOPS = 2 * K * H * S + 2 * H * N * S
+
+F32 = mybir.dt.float32
+BF16 = mybir.dt.bfloat16
+I32 = mybir.dt.int32
+U32 = mybir.dt.uint32
+U16 = mybir.dt.uint16
+U8 = mybir.dt.uint8
+FP8X4 = mybir.dt.float8_e4m3fn_x4
+GELU = mybir.ActivationFunctionType.Gelu_apprx_tanh
+COPY = mybir.ActivationFunctionType.Copy
+
+P = 128
+PACK = 4
+BANK = 512
+CHUNK = 128
+SLICE = 256
+
+
+def tile_picked_zappnp_gelu_po_kernel(
+    tc, x_words, x_scales, w1, w2, gate, gate2, offs, cen, pos1, pos2, nxt1, nxt2, root, out_0, out_1, out_2
+):
+    nc = tc.nc
+    with ExitStack() as ctx:
+        sb = ctx.enter_context(tc.tile_pool(name="sb", bufs=1))
+        psum = ctx.enter_context(tc.psum_pool(name="psum", bufs=1))
+
+        def bank(b, name):
+            return psum.tile([P, BANK], F32, name=name, tag=f"bank{b}")
+
+        def load_list(src, name):
+            tile = sb.tile(list(src.shape), U16, name=name)
+            nc.sync.dma_start(tile[:], src)
+            return tile
+
+        def load_weight(rows, name):
+            raw = sb.tile([P, PACK, 512], F32, name=name)
+            nc.sync.dma_start(out=raw[:], in_=rows.rearrange("(p j) c -> p j c", j=PACK))
+            return raw
+
+        def load_words(g):
+            tile = sb.tile([P, T], I32, name=f"x_win{g}")
+            nc.sync.dma_start(out=tile[:], in_=x_words[g].rearrange("p n r -> p (n r)").bitcast(I32))
+            return tile
+
+        offs_sb = load_list(offs, "offs_sb")
+        w1_raw0 = load_weight(w1[0:512, :], "w1_raw0")
+        xs_win = sb.tile([P, T], U8, name="xs_win")
+        nc.vector.memset(xs_win[:].bitcast(I32), 0)
+        for q in range(4):
+            nc.sync.dma_start(
+                out=xs_win[32 * q : 32 * q + 8, :].bitcast(I32), in_=x_scales[:, 4 * q : 4 * q + 4, :].bitcast(I32)
+            )
+        x_win0 = load_words(0)
+        w1_raw1 = load_weight(w1[512:1024, :], "w1_raw1")
+        x_win1 = load_words(1)
+        w2_raw = load_weight(w2, "w2_raw")
+        pos1_sb = load_list(pos1, "pos1_sb")
+        pos2_sb = load_list(pos2, "pos2_sb")
+        cen_sb = load_list(cen, "cen_sb")
+        root_sb = load_list(root, "root_sb")
+        gate_col = sb.tile([P, 4, 8], F32, name="gate_col")
+        with nc.allow_non_contiguous_dma(reason="one gate value a partition"):
+            for d in range(2):
+                nc.sync.dma_start(out=gate_col[:, d, 0:4], in_=gate[d, 0].rearrange("(b p) -> p b", p=P))
+            for d in range(2):
+                nc.sync.dma_start(out=gate_col[:, 2 + d, 0:2], in_=gate2[d, 0].rearrange("(b p) -> p b", p=P))
+        nxt1_sb = load_list(nxt1, "nxt1_sb")
+        nxt2_sb = load_list(nxt2, "nxt2_sb")
+
+        ident = sb.tile([P, P], F32, name="ident")
+        make_identity(nc, ident[:])
+
+        warm = sb.tile([P, 8], F32, name="warm")
+        nc.gpsimd.memset(warm[:], 0.0)
+        warm_out = sb.tile([P, 8], F32, name="warm_out")
+        nc.scalar.activation(warm_out[:], warm[:], GELU)
+
+        def cast_pair(engine, raw, u, name):
+            grouped = sb.tile([P, 2 * P * PACK], BF16, name=name, align_bytes=64)
+            src = raw[:].rearrange("p j (m t) -> p m j t", t=4)[:, :, :, 2 * u : 2 * u + 2]
+            dst = grouped[:].rearrange("p (t m j) -> p m j t", t=2, j=PACK)
+            if engine == "vector":
+                nc.vector.tensor_copy(out=dst, in_=src)
+            else:
+                nc.scalar.copy(out=dst, in_=src)
+            return grouped
+
+        def quantize(grouped, name):
+            width = grouped.shape[1] // PACK
+            codes = sb.tile([P, width], U32, name=name + "_codes", align_bytes=64)
+            scales = sb.tile([P, width], U8, name=name + "_scales", align_bytes=64)
+            nc.vector.quantize_mx(out=codes[:].bitcast(FP8X4), scales=scales[:], in_=grouped[:])
+            return codes, scales
+
+        def stationary(pairs, t):
+            codes, scales = pairs[t // 2]
+            cols = slice(P * (t % 2), P * (t % 2 + 1))
+            return dict(lhsT=codes[:, cols].bitcast(FP8X4), lhsT_scale=scales[:, cols])
+
+        xs = sb.tile([P, S], U8, name="xs", align_bytes=64)
+        xg = [sb.tile([P, S], U32, name=f"xg{g}", align_bytes=64) for g in range(2)]
+
+        def gather_words(g, win, s):
+            nc.vector.tensor_copy(
+                xg[g][:, SLICE * s : SLICE * (s + 1)], win[:].bitcast(U32).indirect(offs_sb[:, 16 * s : 16 * (s + 1)])
+            )
+
+        nc.vector.tensor_copy(xs[:], xs_win[:].indirect(offs_sb[:]))
+        w1_bf0 = [cast_pair("scalar", w1_raw0, u, f"w1_bf0{u}") for u in range(2)]
+        w1_q0 = [quantize(w1_bf0[u], f"w1_0{u}") for u in range(2)]
+        for s in range(S // SLICE):
+            gather_words(0, x_win0, s)
+
+        h_ps = [bank(c, f"h_ps{c}") for c in range(S // CHUNK)]
+
+        def layer1(g, wq, c):
+            cols = slice(CHUNK * c, CHUNK * (c + 1))
+            for t in range(4):
+                nc.tensor.matmul_mx(
+                    out=h_ps[c][:, CHUNK * t : CHUNK * (t + 1)],
+                    rhs=xg[g][:, cols].bitcast(FP8X4),
+                    rhs_scale=xs[4 * g : P, cols],
+                    start=(g == 0 and t == 0),
+                    stop=(g == 1 and t == 3),
+                    **stationary(wq, t),
+                )
+
+        for c in range(S // CHUNK):
+            layer1(0, w1_q0, c)
+
+        w1_bf1 = [cast_pair("vector", w1_raw1, 0, "w1_bf10"), cast_pair("scalar", w1_raw1, 1, "w1_bf11")]
+        w1_q1 = [quantize(w1_bf1[u], f"w1_1{u}") for u in range(2)]
+        for s in range(S // SLICE):
+            gather_words(1, x_win1, s)
+
+        h_bf = []
+        for c in range(S // CHUNK):
+            layer1(1, w1_q1, c)
+            hb = sb.tile([P, CHUNK * PACK], BF16, name=f"h_bf{c}", align_bytes=64)
+            nc.scalar.activation(
+                hb[:].rearrange("p (n t) -> p n t", t=4), h_ps[c][:].rearrange("p (t n) -> p n t", t=4), GELU
+            )
+            h_bf.append(hb)
+
+        w2_q = [quantize(cast_pair("vector", w2_raw, 0, "w2_bf0"), "w2_0")]
+
+        h_codes = sb.tile([P, S], U32, name="h_codes", align_bytes=64)
+        h_scales = sb.tile([P, S], U8, name="h_scales", align_bytes=64)
+        y = [sb.tile([P, S], F32, name=f"y{t}") for t in range(4)]
+
+        def layer2(t, acc, cols):
+            nc.tensor.matmul_mx(
+                out=acc, rhs=h_codes[:, cols].bitcast(FP8X4), rhs_scale=h_scales[:, cols],
+                start=True, stop=True, **stationary(w2_q, t),
+            )
+
+        for b, (c0, c1) in enumerate([(0, 4), (4, 7), (7, 8)]):
+            acc = bank(b, f"y0_ps{b}")
+            for c in range(c0, c1):
+                cols = slice(CHUNK * c, CHUNK * (c + 1))
+                nc.vector.quantize_mx(out=h_codes[:, cols].bitcast(FP8X4), scales=h_scales[:, cols], in_=h_bf[c][:])
+                layer2(0, acc[:, CHUNK * (c - c0) : CHUNK * (c - c0 + 1)], cols)
+            nc.vector.tensor_copy(out=y[0][:, CHUNK * c0 : CHUNK * c1], in_=acc[:, 0 : CHUNK * (c1 - c0)])
+
+        def second_layer_tile(t, banks):
+            for half in range(2):
+                cols = slice(BANK * half, BANK * (half + 1))
+                acc = bank(banks[half], f"y{t}_ps{half}")
+                layer2(t, acc[:], cols)
+                nc.scalar.copy(out=y[t][:, cols], in_=acc[:])
+
+        second_layer_tile(1, (3, 4))
+        w2_q.append(quantize(cast_pair("scalar", w2_raw, 1, "w2_bf1"), "w2_1"))
+        second_layer_tile(2, (5, 6))
+        second_layer_tile(3, (3, 4))
+
+        def gather(window, offsets, name):
+            picked = sb.tile([P, 16 * offsets.shape[1]], F32, name=name)
+            nc.vector.tensor_copy(picked[:], window[:].indirect(offsets[:]))
+            return picked
+
+        def turn(acc, picked):
+            for b in range(picked.shape[1] // P):
+                nc.tensor.transpose(acc[:, P * b : P * (b + 1)], picked[:, P * b : P * (b + 1)], ident[:])
+
+        def turned(picked, b_idx, name, gate_row):
+            width = picked.shape[1]
+            acc = bank(b_idx, name + "_ps")
+            turn(acc, picked)
+            res = sb.tile([P, width], F32, name=name)
+            if gate_row is None:
+                nc.scalar.activation(res[:], acc[:, 0:width], COPY, scale=0.25)
+            else:
+                for b in range(width // P):
+                    nc.scalar.activation(
+                        res[:, P * b : P * (b + 1)], acc[:, P * b : P * (b + 1)], COPY,
+                        scale=gate_col[:, gate_row, b : b + 1],
+                    )
+            return res
+
+        def sum_back(terms, b_idx, name, dst):
+            width = terms[0].shape[1]
+            acc = bank(b_idx, name)
+            for b in range(width // P):
+                for i, term in enumerate(terms):
+                    nc.tensor.matmul(
+                        acc[:, P * b : P * (b + 1)], lhsT=term[:, P * b : P * (b + 1)], rhs=ident[:],
+                        start=(i == 0), stop=(i == len(terms) - 1), is_transpose=True,
+                    )
+            nc.scalar.activation(dst, acc[:, 0:width], COPY, scale=0.8)
+
+        z, own = [], []
+        for t in range(4):
+            a = turned(gather(y[t], pos1_sb, f"a{t}"), 0, f"aT{t}", 0)
+            b = turned(gather(y[t], pos2_sb, f"b{t}"), 1, f"bT{t}", 1)
+            c = turned(gather(y[t], cen_sb, f"c{t}"), 2, f"cT{t}", None)
+            zt = sb.tile([P, V], F32, name=f"z{t}")
+            sum_back([a, b, c], 7, f"z_ps{t}", zt[:])
+            z.append(zt)
+            own.append(turned(gather(y[t], root_sb, f"r{t}"), 6, f"rT{t}", None))
+
+        res = sb.tile([P, 4, U], F32, name="res")
+        out_rows = out_0.rearrange("(p t) x -> p t x", t=4)
+        for t in range(4):
+            d = turned(gather(z[t], nxt1_sb, f"d{t}"), (0, 2)[t % 2], f"dT{t}", 2)
+            e = turned(gather(z[t], nxt2_sb, f"e{t}"), (1, 3)[t % 2], f"eT{t}", 3)
+            sum_back([own[t], d, e], (4, 5)[t % 2], f"o_ps{t}", res[:, t, :])
+            nc.sync.dma_start(out=out_rows[:, t, :], in_=res[:, t, :])
+
+        res_bf = sb.tile([P, U * PACK], BF16, name="res_bf", align_bytes=64)
+        nc.vector.tensor_copy(
+            out=res_bf[:].rearrange("p (c i t) -> p c t i", i=4, t=4),
+            in_=res[:].rearrange("p t (c i) -> p c t i", i=4),
+        )
+        o_codes, o_scales = quantize(res_bf, "o")
+        nc.sync.dma_start(out=out_1[0].rearrange("p n r -> p (n r)").bitcast(I32), in_=o_codes[:].bitcast(I32))
+        for q in range(4):
+            eng = nc.scalar if q % 2 == 0 else nc.sync
+            eng.dma_start(
+                out=out_2[0, 4 * q : 4 * q + 4, :].bitcast(I32), in_=o_scales[32 * q : 32 * q + 4, :].bitcast(I32)
+            )

@@ -16,6 +16,10 @@ FP8X4 = mybir.dt.float8_e4m3fn_x4
 GELU = mybir.ActivationFunctionType.Gelu_apprx_tanh
 COPY = mybir.ActivationFunctionType.Copy
 
+MULT = mybir.AluOpType.mult
+ADD = mybir.AluOpType.add
+
+CFG = {"s1":[[0,1,2,3],[0,1,2,4],[0,1,2,3],[0,1,2,4]],"s2":[[0,1],[0,1],[0,1]],"y":[[4,3],[2,4],[3,2]],"o":[5,6,7],"r":[2,2,2],"cv":[False,False,True,True],"rv":[False,False,True],"tag":1,"r3":False,"hb":4,"y0":[5,6,7]}
 P = 128
 PACK = 4
 BANK = 512
@@ -49,20 +53,21 @@ def tile_picked_zappnp_gelu_po_kernel(
             nc.sync.dma_start(out=tile[:], in_=x_words[g].rearrange("p n r -> p (n r)").bitcast(I32))
             return tile
 
-        offs_sb = load_list(offs, "offs_sb")
-        w1_raw0 = load_weight(w1[0:512, :], "w1_raw0")
         xs_win = sb.tile([P, T], U8, name="xs_win")
-        nc.vector.memset(xs_win[:].bitcast(I32), 0)
+        nc.vector.memset(xs_win[:, 0:1280].bitcast(I32), 0)
+        nc.gpsimd.memset(xs_win[:, 1280:T].bitcast(I32), 0)
         for q in range(4):
             nc.sync.dma_start(
                 out=xs_win[32 * q : 32 * q + 8, :].bitcast(I32), in_=x_scales[:, 4 * q : 4 * q + 4, :].bitcast(I32)
             )
+        offs_sb = load_list(offs, "offs_sb")
         x_win0 = load_words(0)
+        pos1_sb = load_list(pos1, "pos1_sb")
+        pos2_sb = load_list(pos2, "pos2_sb")
+        w1_raw0 = load_weight(w1[0:512, :], "w1_raw0")
         w1_raw1 = load_weight(w1[512:1024, :], "w1_raw1")
         x_win1 = load_words(1)
         w2_raw = load_weight(w2, "w2_raw")
-        pos1_sb = load_list(pos1, "pos1_sb")
-        pos2_sb = load_list(pos2, "pos2_sb")
         cen_sb = load_list(cen, "cen_sb")
         root_sb = load_list(root, "root_sb")
         gate_col = sb.tile([P, 4, 8], F32, name="gate_col")
@@ -73,6 +78,8 @@ def tile_picked_zappnp_gelu_po_kernel(
                 nc.sync.dma_start(out=gate_col[:, 2 + d, 0:2], in_=gate2[d, 0].rearrange("(b p) -> p b", p=P))
         nxt1_sb = load_list(nxt1, "nxt1_sb")
         nxt2_sb = load_list(nxt2, "nxt2_sb")
+        gate2_rows = sb.tile([P, 2, U], F32, name="gate2_rows")
+        nc.sync.dma_start(out=gate2_rows[:], in_=gate2.rearrange("d p x -> p d x"))
 
         ident = sb.tile([P, P], F32, name="ident")
         make_identity(nc, ident[:])
@@ -83,7 +90,7 @@ def tile_picked_zappnp_gelu_po_kernel(
         nc.scalar.activation(warm_out[:], warm[:], GELU)
 
         def cast_pair(engine, raw, u, name):
-            grouped = sb.tile([P, 2 * P * PACK], BF16, name=name, align_bytes=64)
+            grouped = sb.tile([P, 2 * P * PACK], BF16, name=name, tag=name, align_bytes=64)
             src = raw[:].rearrange("p j (m t) -> p m j t", t=4)[:, :, :, 2 * u : 2 * u + 2]
             dst = grouped[:].rearrange("p (t m j) -> p m j t", t=2, j=PACK)
             if engine == "vector":
@@ -118,7 +125,7 @@ def tile_picked_zappnp_gelu_po_kernel(
         for s in range(S // SLICE):
             gather_words(0, x_win0, s)
 
-        h_ps = [bank(c, f"h_ps{c}") for c in range(S // CHUNK)]
+        h_ps = {}
 
         def layer1(g, wq, c):
             cols = slice(CHUNK * c, CHUNK * (c + 1))
@@ -132,9 +139,6 @@ def tile_picked_zappnp_gelu_po_kernel(
                     **stationary(wq, t),
                 )
 
-        for c in range(S // CHUNK):
-            layer1(0, w1_q0, c)
-
         w1_bf1 = [cast_pair("vector", w1_raw1, 0, "w1_bf10"), cast_pair("scalar", w1_raw1, 1, "w1_bf11")]
         w1_q1 = [quantize(w1_bf1[u], f"w1_1{u}") for u in range(2)]
         for s in range(S // SLICE):
@@ -142,6 +146,8 @@ def tile_picked_zappnp_gelu_po_kernel(
 
         h_bf = []
         for c in range(S // CHUNK):
+            h_ps[c] = bank(c % CFG["hb"], f"h_ps{c}")
+            layer1(0, w1_q0, c)
             layer1(1, w1_q1, c)
             hb = sb.tile([P, CHUNK * PACK], BF16, name=f"h_bf{c}", align_bytes=64)
             nc.scalar.activation(
@@ -162,41 +168,37 @@ def tile_picked_zappnp_gelu_po_kernel(
             )
 
         for b, (c0, c1) in enumerate([(0, 4), (4, 7), (7, 8)]):
-            acc = bank(b, f"y0_ps{b}")
+            acc = bank(CFG["y0"][b], f"y0_ps{b}")
             for c in range(c0, c1):
                 cols = slice(CHUNK * c, CHUNK * (c + 1))
                 nc.vector.quantize_mx(out=h_codes[:, cols].bitcast(FP8X4), scales=h_scales[:, cols], in_=h_bf[c][:])
                 layer2(0, acc[:, CHUNK * (c - c0) : CHUNK * (c - c0 + 1)], cols)
-            nc.vector.tensor_copy(out=y[0][:, CHUNK * c0 : CHUNK * c1], in_=acc[:, 0 : CHUNK * (c1 - c0)])
+            nc.vector.tensor_scalar_mul(y[0][:, CHUNK * c0 : CHUNK * c1], acc[:, 0 : CHUNK * (c1 - c0)], 0.2)
 
         def second_layer_tile(t, banks):
             for half in range(2):
                 cols = slice(BANK * half, BANK * (half + 1))
                 acc = bank(banks[half], f"y{t}_ps{half}")
                 layer2(t, acc[:], cols)
-                nc.scalar.copy(out=y[t][:, cols], in_=acc[:])
+                nc.scalar.activation(y[t][:, cols], acc[:], COPY, scale=0.2)
 
-        second_layer_tile(1, (3, 4))
         w2_q.append(quantize(cast_pair("scalar", w2_raw, 1, "w2_bf1"), "w2_1"))
-        second_layer_tile(2, (5, 6))
-        second_layer_tile(3, (3, 4))
+        for t in range(1, 4):
+            second_layer_tile(t, CFG["y"][t - 1])
 
-        def gather(window, offsets, name):
-            picked = sb.tile([P, 16 * offsets.shape[1]], F32, name=name)
+        def gather(window, offsets, name, tag=""):
+            picked = sb.tile([P, 16 * offsets.shape[1]], F32, name=name, tag=tag, align_bytes=64)
             nc.vector.tensor_copy(picked[:], window[:].indirect(offsets[:]))
             return picked
 
-        def turn(acc, picked):
-            for b in range(picked.shape[1] // P):
-                nc.tensor.transpose(acc[:, P * b : P * (b + 1)], picked[:, P * b : P * (b + 1)], ident[:])
-
-        def turned(picked, b_idx, name, gate_row):
+        def turned(picked, b_idx, name, gate_row, factor=None):
             width = picked.shape[1]
             acc = bank(b_idx, name + "_ps")
-            turn(acc, picked)
+            for b in range(width // P):
+                nc.tensor.transpose(acc[:, P * b : P * (b + 1)], picked[:, P * b : P * (b + 1)], ident[:])
             res = sb.tile([P, width], F32, name=name)
             if gate_row is None:
-                nc.scalar.activation(res[:], acc[:, 0:width], COPY, scale=0.25)
+                nc.scalar.activation(res[:], acc[:, 0:width], COPY, scale=factor)
             else:
                 for b in range(width // P):
                     nc.scalar.activation(
@@ -205,40 +207,83 @@ def tile_picked_zappnp_gelu_po_kernel(
                     )
             return res
 
-        def sum_back(terms, b_idx, name, dst):
-            width = terms[0].shape[1]
-            acc = bank(b_idx, name)
-            for b in range(width // P):
-                for i, term in enumerate(terms):
-                    nc.tensor.matmul(
-                        acc[:, P * b : P * (b + 1)], lhsT=term[:, P * b : P * (b + 1)], rhs=ident[:],
-                        start=(i == 0), stop=(i == len(terms) - 1), is_transpose=True,
-                    )
-            nc.scalar.activation(dst, acc[:, 0:width], COPY, scale=0.8)
-
-        z, own = [], []
-        for t in range(4):
-            a = turned(gather(y[t], pos1_sb, f"a{t}"), 0, f"aT{t}", 0)
-            b = turned(gather(y[t], pos2_sb, f"b{t}"), 1, f"bT{t}", 1)
-            c = turned(gather(y[t], cen_sb, f"c{t}"), 2, f"cT{t}", None)
-            zt = sb.tile([P, V], F32, name=f"z{t}")
-            sum_back([a, b, c], 7, f"z_ps{t}", zt[:])
-            z.append(zt)
-            own.append(turned(gather(y[t], root_sb, f"r{t}"), 6, f"rT{t}", None))
+        def add_back(acc, term, first, last):
+            blocks = term.shape[1] // P
+            for b in range(blocks):
+                nc.tensor.matmul(
+                    acc[:, P * b : P * (b + 1)], lhsT=term[:, P * b : P * (b + 1)], rhs=ident[:],
+                    start=(first and b == 0), stop=(last and b == blocks - 1), is_transpose=True,
+                )
 
         res = sb.tile([P, 4, U], F32, name="res")
         out_rows = out_0.rearrange("(p t) x -> p t x", t=4)
-        for t in range(4):
-            d = turned(gather(z[t], nxt1_sb, f"d{t}"), (0, 2)[t % 2], f"dT{t}", 2)
-            e = turned(gather(z[t], nxt2_sb, f"e{t}"), (1, 3)[t % 2], f"eT{t}", 3)
-            sum_back([own[t], d, e], (4, 5)[t % 2], f"o_ps{t}", res[:, t, :])
+        z, o_ps = {}, {}
+
+        own = {}
+        res_bf = sb.tile([P, U * PACK], BF16, name="res_bf", align_bytes=64)
+
+        def round_pair(engine_copy, u):
+            engine_copy(
+                out=res_bf[:].rearrange("p (x t) -> p x t", t=4)[:, :, 2 * u : 2 * u + 2],
+                in_=res[:, 2 * u : 2 * u + 2, :].rearrange("p t x -> p x t"),
+            )
+
+        def first_step(t):
+            ba, bb, bc, bz = CFG["s1"][t]
+            on_vector = CFG["cv"][t]
+            a = turned(gather(y[t], pos1_sb, f"a{t}", tag="w2_bf1" if (t == 0 and CFG["tag"] == 0) else ""), ba, f"aT{t}", 0)
+            acc = bank(bz, f"z_ps{t}")
+            add_back(acc, a, True, False)
+            b = turned(gather(y[t], pos2_sb, f"b{t}", tag="w2_bf1" if (t == 0 and CFG["tag"] == 1) else ""), bb, f"bT{t}", 1)
+            add_back(acc, b, False, on_vector)
+            c = gather(y[t], cen_sb, f"c{t}")
+            z[t] = sb.tile([P, V], F32, name=f"z{t}", tag=f"z{t}", align_bytes=64)
+            if on_vector:
+                nc.vector.scalar_tensor_tensor(z[t][:], acc[:], 4.0, c[:], MULT, ADD)
+            else:
+                add_back(acc, turned(c, bc, f"cT{t}", None, 0.25), False, True)
+                nc.scalar.activation(z[t][:], acc[:], COPY, scale=4.0)
+
+        def root_term(t):
+            r = gather(y[t], root_sb, f"r{t}")
+            if CFG["rv"][t]:
+                own[t] = r
+            else:
+                o_ps[t] = bank(CFG["o"][t], f"o_ps{t}")
+                add_back(o_ps[t], turned(r, CFG["r"][t], f"rT{t}", None, 1.25), True, False)
+
+        def second_step(t):
+            bd, be = CFG["s2"][t]
+            d = turned(gather(z[t], nxt1_sb, f"d{t}"), bd, f"dT{t}", 2)
+            if CFG["rv"][t]:
+                o_ps[t] = bank(CFG["o"][t], f"o_ps{t}")
+            add_back(o_ps[t], d, CFG["rv"][t], False)
+            add_back(o_ps[t], turned(gather(z[t], nxt2_sb, f"e{t}"), be, f"eT{t}", 3), False, True)
+            if CFG["rv"][t]:
+                nc.vector.scalar_tensor_tensor(res[:, t, :], o_ps[t][:, 0:U], 0.8, own[t][:], MULT, ADD)
+            else:
+                nc.scalar.activation(res[:, t, :], o_ps[t][:, 0:U], COPY, scale=0.8)
             nc.sync.dma_start(out=out_rows[:, t, :], in_=res[:, t, :])
 
-        res_bf = sb.tile([P, U * PACK], BF16, name="res_bf", align_bytes=64)
-        nc.vector.tensor_copy(
-            out=res_bf[:].rearrange("p (c i t) -> p c t i", i=4, t=4),
-            in_=res[:].rearrange("p t (c i) -> p c t i", i=4),
-        )
+        for t in range(4):
+            first_step(t)
+            if t < 3:
+                root_term(t)
+        for t in range(3):
+            second_step(t)
+            if t == 1:
+                round_pair(nc.scalar.copy, 0)
+
+        r = gather(y[3], root_sb, "r3", tag="z2" if CFG["r3"] else "")
+        d = sb.tile([P, U], F32, name="d3")
+        nc.vector.tensor_tensor(d[:], z[3][:].indirect(nxt1_sb[:]), gate2_rows[:, 0, :], MULT)
+        e = sb.tile([P, U], F32, name="e3")
+        nc.vector.tensor_tensor(e[:], z[3][:].indirect(nxt2_sb[:]), gate2_rows[:, 1, :], MULT)
+        part = sb.tile([P, U], F32, name="part")
+        nc.vector.scalar_tensor_tensor(part[:], d[:], 0.8, r[:], MULT, ADD)
+        nc.vector.scalar_tensor_tensor(res[:, 3, :], e[:], 0.8, part[:], MULT, ADD)
+        nc.sync.dma_start(out=out_rows[:, 3, :], in_=res[:, 3, :])
+        round_pair(nc.vector.tensor_copy, 1)
         o_codes, o_scales = quantize(res_bf, "o")
         nc.sync.dma_start(out=out_1[0].rearrange("p n r -> p (n r)").bitcast(I32), in_=o_codes[:].bitcast(I32))
         for q in range(4):

@@ -15,16 +15,15 @@ U8 = mybir.dt.uint8
 FP8X4 = mybir.dt.float8_e4m3fn_x4
 GELU = mybir.ActivationFunctionType.Gelu_apprx_tanh
 COPY = mybir.ActivationFunctionType.Copy
-
 MULT = mybir.AluOpType.mult
 ADD = mybir.AluOpType.add
 
-CFG = {"s1":[[0,1,2,3],[0,1,2,4],[0,1,2,3],[0,1,2,4]],"s2":[[0,1],[0,1],[0,1]],"y":[[4,3],[2,4],[3,2]],"o":[5,6,7],"r":[2,2,2],"cv":[False,False,True,True],"rv":[False,False,True],"tag":1,"r3":False,"hb":4,"y0":[5,6,7]}
 P = 128
 PACK = 4
 BANK = 512
 CHUNK = 128
 SLICE = 256
+H_BANKS = 4
 
 
 def tile_picked_zappnp_gelu_po_kernel(
@@ -62,41 +61,46 @@ def tile_picked_zappnp_gelu_po_kernel(
             )
         offs_sb = load_list(offs, "offs_sb")
         x_win0 = load_words(0)
-        pos1_sb = load_list(pos1, "pos1_sb")
-        pos2_sb = load_list(pos2, "pos2_sb")
+        gate_col = sb.tile([P, 2, 4], F32, name="gate_col")
+        gate2_col = sb.tile([P, 2, 2], F32, name="gate2_col")
+        with nc.allow_non_contiguous_dma(reason="a few gate values a partition"):
+            nc.sync.dma_start(out=gate_col[:], in_=gate[:, 0, :].rearrange("d (p b) -> p d b", p=P))
+            nc.sync.dma_start(out=gate2_col[:], in_=gate2[:, 0, :].rearrange("d (p b) -> p d b", p=P))
         w1_raw0 = load_weight(w1[0:512, :], "w1_raw0")
         w1_raw1 = load_weight(w1[512:1024, :], "w1_raw1")
         x_win1 = load_words(1)
         w2_raw = load_weight(w2, "w2_raw")
+        pos1_sb = load_list(pos1, "pos1_sb")
+        pos2_sb = load_list(pos2, "pos2_sb")
         cen_sb = load_list(cen, "cen_sb")
         root_sb = load_list(root, "root_sb")
-        gate_col = sb.tile([P, 4, 8], F32, name="gate_col")
-        with nc.allow_non_contiguous_dma(reason="one gate value a partition"):
-            for d in range(2):
-                nc.sync.dma_start(out=gate_col[:, d, 0:4], in_=gate[d, 0].rearrange("(b p) -> p b", p=P))
-            for d in range(2):
-                nc.sync.dma_start(out=gate_col[:, 2 + d, 0:2], in_=gate2[d, 0].rearrange("(b p) -> p b", p=P))
         nxt1_sb = load_list(nxt1, "nxt1_sb")
         nxt2_sb = load_list(nxt2, "nxt2_sb")
-        gate2_rows = sb.tile([P, 2, U], F32, name="gate2_rows")
-        nc.sync.dma_start(out=gate2_rows[:], in_=gate2.rearrange("d p x -> p d x"))
 
         ident = sb.tile([P, P], F32, name="ident")
         make_identity(nc, ident[:])
 
-        warm = sb.tile([P, 8], F32, name="warm")
-        nc.gpsimd.memset(warm[:], 0.0)
-        warm_out = sb.tile([P, 8], F32, name="warm_out")
-        nc.scalar.activation(warm_out[:], warm[:], GELU)
+        def spread(col, acc, factor, name):
+            blocks = col.shape[1]
+            for b in range(blocks):
+                nc.tensor.transpose(acc[:, P * b : P * (b + 1)], col[:, b : b + 1].to_broadcast([P, P]), ident[:])
+            row = sb.tile([P, P * blocks], F32, name=name, tag=name)
+            nc.scalar.activation(
+                row[:].rearrange("p (n b) -> p n b", b=blocks),
+                acc[:, 0 : P * blocks].rearrange("p (b n) -> p n b", b=blocks),
+                COPY,
+                scale=factor,
+            )
+            return row
 
-        def cast_pair(engine, raw, u, name):
-            grouped = sb.tile([P, 2 * P * PACK], BF16, name=name, tag=name, align_bytes=64)
+        gate_row = [spread(gate_col[:, d, :], bank(4 + d, f"gate_ps{d}"), 4.0, f"gate_row{d}") for d in range(2)]
+        gate2_row = [spread(gate2_col[:, d, :], bank(6 + d, f"gate2_ps{d}"), 0.8, f"gate2_row{d}") for d in range(2)]
+
+        def cast_pair(engine_copy, raw, u, name):
+            grouped = sb.tile([P, 2 * P * PACK], BF16, name=name, align_bytes=64)
             src = raw[:].rearrange("p j (m t) -> p m j t", t=4)[:, :, :, 2 * u : 2 * u + 2]
             dst = grouped[:].rearrange("p (t m j) -> p m j t", t=2, j=PACK)
-            if engine == "vector":
-                nc.vector.tensor_copy(out=dst, in_=src)
-            else:
-                nc.scalar.copy(out=dst, in_=src)
+            engine_copy(out=dst, in_=src)
             return grouped
 
         def quantize(grouped, name):
@@ -120,7 +124,7 @@ def tile_picked_zappnp_gelu_po_kernel(
             )
 
         nc.vector.tensor_copy(xs[:], xs_win[:].indirect(offs_sb[:]))
-        w1_bf0 = [cast_pair("scalar", w1_raw0, u, f"w1_bf0{u}") for u in range(2)]
+        w1_bf0 = [cast_pair(nc.scalar.copy, w1_raw0, u, f"w1_bf0{u}") for u in range(2)]
         w1_q0 = [quantize(w1_bf0[u], f"w1_0{u}") for u in range(2)]
         for s in range(S // SLICE):
             gather_words(0, x_win0, s)
@@ -139,14 +143,14 @@ def tile_picked_zappnp_gelu_po_kernel(
                     **stationary(wq, t),
                 )
 
-        w1_bf1 = [cast_pair("vector", w1_raw1, 0, "w1_bf10"), cast_pair("scalar", w1_raw1, 1, "w1_bf11")]
+        w1_bf1 = [cast_pair(nc.vector.tensor_copy, w1_raw1, 0, "w1_bf10"), cast_pair(nc.scalar.copy, w1_raw1, 1, "w1_bf11")]
         w1_q1 = [quantize(w1_bf1[u], f"w1_1{u}") for u in range(2)]
         for s in range(S // SLICE):
             gather_words(1, x_win1, s)
 
         h_bf = []
         for c in range(S // CHUNK):
-            h_ps[c] = bank(c % CFG["hb"], f"h_ps{c}")
+            h_ps[c] = bank(c % H_BANKS, f"h_ps{c}")
             layer1(0, w1_q0, c)
             layer1(1, w1_q1, c)
             hb = sb.tile([P, CHUNK * PACK], BF16, name=f"h_bf{c}", align_bytes=64)
@@ -155,7 +159,7 @@ def tile_picked_zappnp_gelu_po_kernel(
             )
             h_bf.append(hb)
 
-        w2_q = [quantize(cast_pair("vector", w2_raw, 0, "w2_bf0"), "w2_0")]
+        w2_q = [quantize(cast_pair(nc.vector.tensor_copy, w2_raw, 0, "w2_bf0"), "w2_0")]
 
         h_codes = sb.tile([P, S], U32, name="h_codes", align_bytes=64)
         h_scales = sb.tile([P, S], U8, name="h_scales", align_bytes=64)
@@ -168,59 +172,36 @@ def tile_picked_zappnp_gelu_po_kernel(
             )
 
         for b, (c0, c1) in enumerate([(0, 4), (4, 7), (7, 8)]):
-            acc = bank(CFG["y0"][b], f"y0_ps{b}")
+            acc = bank(5 + b, f"y0_ps{b}")
             for c in range(c0, c1):
                 cols = slice(CHUNK * c, CHUNK * (c + 1))
                 nc.vector.quantize_mx(out=h_codes[:, cols].bitcast(FP8X4), scales=h_scales[:, cols], in_=h_bf[c][:])
                 layer2(0, acc[:, CHUNK * (c - c0) : CHUNK * (c - c0 + 1)], cols)
             nc.vector.tensor_scalar_mul(y[0][:, CHUNK * c0 : CHUNK * c1], acc[:, 0 : CHUNK * (c1 - c0)], 0.2)
 
-        def second_layer_tile(t, banks):
+        def second_layer_tile(t):
             for half in range(2):
                 cols = slice(BANK * half, BANK * (half + 1))
-                acc = bank(banks[half], f"y{t}_ps{half}")
+                acc = bank((2 * t + 2 + half) % 5, f"y{t}_ps{half}")
                 layer2(t, acc[:], cols)
                 nc.scalar.activation(y[t][:, cols], acc[:], COPY, scale=0.2)
 
-        w2_q.append(quantize(cast_pair("scalar", w2_raw, 1, "w2_bf1"), "w2_1"))
-        for t in range(1, 4):
-            second_layer_tile(t, CFG["y"][t - 1])
+        second_layer_tile(1)
+        w2_q.append(quantize(cast_pair(nc.scalar.copy, w2_raw, 1, "w2_bf1"), "w2_1"))
+        for t in range(2, 4):
+            second_layer_tile(t)
 
-        def gather(window, offsets, name, tag=""):
-            picked = sb.tile([P, 16 * offsets.shape[1]], F32, name=name, tag=tag, align_bytes=64)
-            nc.vector.tensor_copy(picked[:], window[:].indirect(offsets[:]))
-            return picked
-
-        def turned(picked, b_idx, name, gate_row, factor=None):
-            width = picked.shape[1]
-            acc = bank(b_idx, name + "_ps")
-            for b in range(width // P):
-                nc.tensor.transpose(acc[:, P * b : P * (b + 1)], picked[:, P * b : P * (b + 1)], ident[:])
-            res = sb.tile([P, width], F32, name=name)
-            if gate_row is None:
-                nc.scalar.activation(res[:], acc[:, 0:width], COPY, scale=factor)
-            else:
-                for b in range(width // P):
-                    nc.scalar.activation(
-                        res[:, P * b : P * (b + 1)], acc[:, P * b : P * (b + 1)], COPY,
-                        scale=gate_col[:, gate_row, b : b + 1],
-                    )
-            return res
-
-        def add_back(acc, term, first, last):
-            blocks = term.shape[1] // P
-            for b in range(blocks):
-                nc.tensor.matmul(
-                    acc[:, P * b : P * (b + 1)], lhsT=term[:, P * b : P * (b + 1)], rhs=ident[:],
-                    start=(first and b == 0), stop=(last and b == blocks - 1), is_transpose=True,
-                )
+        def gather_op(window, offsets, other, op, name, out=None):
+            if out is None:
+                picked = sb.tile([P, 16 * offsets.shape[1]], F32, name=name, tag=name)
+                out = picked[:]
+            nc.vector.tensor_tensor(out, window[:].indirect(offsets[:]), other, op)
+            return out
 
         res = sb.tile([P, 4, U], F32, name="res")
         out_rows = out_0.rearrange("(p t) x -> p t x", t=4)
-        z, o_ps = {}, {}
-
-        own = {}
         res_bf = sb.tile([P, U * PACK], BF16, name="res_bf", align_bytes=64)
+        z = {}
 
         def round_pair(engine_copy, u):
             engine_copy(
@@ -228,61 +209,46 @@ def tile_picked_zappnp_gelu_po_kernel(
                 in_=res[:, 2 * u : 2 * u + 2, :].rearrange("p t x -> p x t"),
             )
 
-        def first_step(t):
-            ba, bb, bc, bz = CFG["s1"][t]
-            on_vector = CFG["cv"][t]
-            a = turned(gather(y[t], pos1_sb, f"a{t}", tag="w2_bf1" if (t == 0 and CFG["tag"] == 0) else ""), ba, f"aT{t}", 0)
-            acc = bank(bz, f"z_ps{t}")
-            add_back(acc, a, True, False)
-            b = turned(gather(y[t], pos2_sb, f"b{t}", tag="w2_bf1" if (t == 0 and CFG["tag"] == 1) else ""), bb, f"bT{t}", 1)
-            add_back(acc, b, False, on_vector)
-            c = gather(y[t], cen_sb, f"c{t}")
-            z[t] = sb.tile([P, V], F32, name=f"z{t}", tag=f"z{t}", align_bytes=64)
-            if on_vector:
-                nc.vector.scalar_tensor_tensor(z[t][:], acc[:], 4.0, c[:], MULT, ADD)
-            else:
-                add_back(acc, turned(c, bc, f"cT{t}", None, 0.25), False, True)
-                nc.scalar.activation(z[t][:], acc[:], COPY, scale=4.0)
+        def add_on_tensor(terms, out, banks, name):
+            blocks = out.shape[1] // P
+            turned = bank(banks[0], name + "_turned")
+            for i, term in enumerate(terms):
+                for b in range(blocks):
+                    nc.tensor.matmul(
+                        turned[:, P * b : P * (b + 1)], lhsT=term[:, P * b : P * (b + 1)], rhs=ident[:],
+                        start=(i == 0 and b == 0), stop=(i == len(terms) - 1 and b == blocks - 1), is_transpose=True,
+                    )
+            total = sb.tile([P, P * blocks], F32, name=name + "_total")
+            nc.scalar.copy(out=total[:], in_=turned[:, 0 : P * blocks])
+            back = bank(banks[1], name + "_back")
+            for b in range(blocks):
+                nc.tensor.transpose(back[:, P * b : P * (b + 1)], total[:, P * b : P * (b + 1)], ident[:])
+            nc.scalar.copy(out=out, in_=back[:, 0 : P * blocks])
 
-        def root_term(t):
-            r = gather(y[t], root_sb, f"r{t}")
-            if CFG["rv"][t]:
-                own[t] = r
-            else:
-                o_ps[t] = bank(CFG["o"][t], f"o_ps{t}")
-                add_back(o_ps[t], turned(r, CFG["r"][t], f"rT{t}", None, 1.25), True, False)
+        def first_step(t):
+            a = gather_op(y[t], pos1_sb, gate_row[0][:], MULT, f"a{t}")
+            b = gather_op(y[t], pos2_sb, gate_row[1][:], MULT, f"b{t}")
+            c = sb.tile([P, V], F32, name=f"c{t}")
+            nc.vector.tensor_copy(c[:], y[t][:].indirect(cen_sb[:]))
+            z[t] = sb.tile([P, V], F32, name=f"z{t}")
+            pair = (5, 6) if t % 2 == 0 else (7, 0)
+            add_on_tensor([a, b, c[:]], z[t][:], pair if t < 2 else pair[::-1], f"z{t}")
 
         def second_step(t):
-            bd, be = CFG["s2"][t]
-            d = turned(gather(z[t], nxt1_sb, f"d{t}"), bd, f"dT{t}", 2)
-            if CFG["rv"][t]:
-                o_ps[t] = bank(CFG["o"][t], f"o_ps{t}")
-            add_back(o_ps[t], d, CFG["rv"][t], False)
-            add_back(o_ps[t], turned(gather(z[t], nxt2_sb, f"e{t}"), be, f"eT{t}", 3), False, True)
-            if CFG["rv"][t]:
-                nc.vector.scalar_tensor_tensor(res[:, t, :], o_ps[t][:, 0:U], 0.8, own[t][:], MULT, ADD)
-            else:
-                nc.scalar.activation(res[:, t, :], o_ps[t][:, 0:U], COPY, scale=0.8)
+            d = gather_op(z[t], nxt1_sb, gate2_row[0][:], MULT, "", out=late[t // 2][:, t % 2, :])
+            e = gather_op(z[t], nxt2_sb, gate2_row[1][:], MULT, "", out=late[2 + t // 2][:, t % 2, :])
+            both = sb.tile([P, U], F32, name=f"both{t}")
+            nc.vector.tensor_tensor(both[:], d, e, ADD)
+            gather_op(y[t], root_sb, both[:], ADD, "", out=res[:, t, :])
             nc.sync.dma_start(out=out_rows[:, t, :], in_=res[:, t, :])
 
         for t in range(4):
             first_step(t)
-            if t < 3:
-                root_term(t)
-        for t in range(3):
+        late = [sb.tile([P, 2, U], F32, name=f"late{i}", tag=tag) for i, tag in enumerate(["gate_row1", "gate_row0", "a3", "a2"])]
+        for t in range(4):
             second_step(t)
             if t == 1:
                 round_pair(nc.scalar.copy, 0)
-
-        r = gather(y[3], root_sb, "r3", tag="z2" if CFG["r3"] else "")
-        d = sb.tile([P, U], F32, name="d3")
-        nc.vector.tensor_tensor(d[:], z[3][:].indirect(nxt1_sb[:]), gate2_rows[:, 0, :], MULT)
-        e = sb.tile([P, U], F32, name="e3")
-        nc.vector.tensor_tensor(e[:], z[3][:].indirect(nxt2_sb[:]), gate2_rows[:, 1, :], MULT)
-        part = sb.tile([P, U], F32, name="part")
-        nc.vector.scalar_tensor_tensor(part[:], d[:], 0.8, r[:], MULT, ADD)
-        nc.vector.scalar_tensor_tensor(res[:, 3, :], e[:], 0.8, part[:], MULT, ADD)
-        nc.sync.dma_start(out=out_rows[:, 3, :], in_=res[:, 3, :])
         round_pair(nc.vector.tensor_copy, 1)
         o_codes, o_scales = quantize(res_bf, "o")
         nc.sync.dma_start(out=out_1[0].rearrange("p n r -> p (n r)").bitcast(I32), in_=o_codes[:].bitcast(I32))

@@ -23,7 +23,7 @@ PACK = 4
 BANK = 512
 CHUNK = 128
 SLICE = 256
-H_BANKS = 4
+H_BANKS = 8
 
 
 def tile_picked_zappnp_gelu_po_kernel(
@@ -53,48 +53,33 @@ def tile_picked_zappnp_gelu_po_kernel(
             return tile
 
         xs_win = sb.tile([P, T], U8, name="xs_win")
-        nc.vector.memset(xs_win[:, 0:1280].bitcast(I32), 0)
-        nc.gpsimd.memset(xs_win[:, 1280:T].bitcast(I32), 0)
+        nc.gpsimd.memset(xs_win[:].bitcast(I32), 0)
         for q in range(4):
             nc.sync.dma_start(
                 out=xs_win[32 * q : 32 * q + 8, :].bitcast(I32), in_=x_scales[:, 4 * q : 4 * q + 4, :].bitcast(I32)
             )
         offs_sb = load_list(offs, "offs_sb")
-        x_win0 = load_words(0)
-        gate_col = sb.tile([P, 2, 4], F32, name="gate_col")
-        gate2_col = sb.tile([P, 2, 2], F32, name="gate2_col")
-        with nc.allow_non_contiguous_dma(reason="a few gate values a partition"):
-            nc.sync.dma_start(out=gate_col[:], in_=gate[:, 0, :].rearrange("d (p b) -> p d b", p=P))
-            nc.sync.dma_start(out=gate2_col[:], in_=gate2[:, 0, :].rearrange("d (p b) -> p d b", p=P))
+        pos1_sb = load_list(pos1, "pos1_sb")
+        pos2_sb = load_list(pos2, "pos2_sb")
         w1_raw0 = load_weight(w1[0:512, :], "w1_raw0")
+        x_win0 = load_words(0)
         w1_raw1 = load_weight(w1[512:1024, :], "w1_raw1")
         x_win1 = load_words(1)
         w2_raw = load_weight(w2, "w2_raw")
-        pos1_sb = load_list(pos1, "pos1_sb")
-        pos2_sb = load_list(pos2, "pos2_sb")
+        gate_row = []
+        for d in range(2):
+            row = sb.tile([P, V], F32, name=f"gate_row{d}")
+            nc.sync.dma_start(out=row[:], in_=gate[d])
+            gate_row.append(row)
         cen_sb = load_list(cen, "cen_sb")
-        root_sb = load_list(root, "root_sb")
         nxt1_sb = load_list(nxt1, "nxt1_sb")
         nxt2_sb = load_list(nxt2, "nxt2_sb")
+        gate2_raw = sb.tile([P, 2, U], F32, name="gate2_raw")
+        nc.sync.dma_start(out=gate2_raw[:], in_=gate2.rearrange("d p x -> p d x"))
+        root_sb = load_list(root, "root_sb")
 
         ident = sb.tile([P, P], F32, name="ident")
         make_identity(nc, ident[:])
-
-        def spread(col, acc, factor, name):
-            blocks = col.shape[1]
-            for b in range(blocks):
-                nc.tensor.transpose(acc[:, P * b : P * (b + 1)], col[:, b : b + 1].to_broadcast([P, P]), ident[:])
-            row = sb.tile([P, P * blocks], F32, name=name, tag=name)
-            nc.scalar.activation(
-                row[:].rearrange("p (n b) -> p n b", b=blocks),
-                acc[:, 0 : P * blocks].rearrange("p (b n) -> p n b", b=blocks),
-                COPY,
-                scale=factor,
-            )
-            return row
-
-        gate_row = [spread(gate_col[:, d, :], bank(4 + d, f"gate_ps{d}"), 4.0, f"gate_row{d}") for d in range(2)]
-        gate2_row = [spread(gate2_col[:, d, :], bank(6 + d, f"gate2_ps{d}"), 0.8, f"gate2_row{d}") for d in range(2)]
 
         def cast_pair(engine_copy, raw, u, name):
             grouped = sb.tile([P, 2 * P * PACK], BF16, name=name, align_bytes=64)
@@ -124,7 +109,7 @@ def tile_picked_zappnp_gelu_po_kernel(
             )
 
         nc.vector.tensor_copy(xs[:], xs_win[:].indirect(offs_sb[:]))
-        w1_bf0 = [cast_pair(nc.scalar.copy, w1_raw0, u, f"w1_bf0{u}") for u in range(2)]
+        w1_bf0 = [cast_pair(nc.vector.tensor_copy, w1_raw0, 0, "w1_bf00"), cast_pair(nc.scalar.copy, w1_raw0, 1, "w1_bf01")]
         w1_q0 = [quantize(w1_bf0[u], f"w1_0{u}") for u in range(2)]
         for s in range(S // SLICE):
             gather_words(0, x_win0, s)
@@ -172,7 +157,7 @@ def tile_picked_zappnp_gelu_po_kernel(
             )
 
         for b, (c0, c1) in enumerate([(0, 4), (4, 7), (7, 8)]):
-            acc = bank(5 + b, f"y0_ps{b}")
+            acc = bank(b, f"y0_ps{b}")
             for c in range(c0, c1):
                 cols = slice(CHUNK * c, CHUNK * (c + 1))
                 nc.vector.quantize_mx(out=h_codes[:, cols].bitcast(FP8X4), scales=h_scales[:, cols], in_=h_bf[c][:])
@@ -182,35 +167,20 @@ def tile_picked_zappnp_gelu_po_kernel(
         def second_layer_tile(t):
             for half in range(2):
                 cols = slice(BANK * half, BANK * (half + 1))
-                acc = bank((2 * t + 2 + half) % 5, f"y{t}_ps{half}")
+                acc = bank((2 * t + 1 + half) % 8, f"y{t}_ps{half}")
                 layer2(t, acc[:], cols)
                 nc.scalar.activation(y[t][:, cols], acc[:], COPY, scale=0.2)
 
-        second_layer_tile(1)
         w2_q.append(quantize(cast_pair(nc.scalar.copy, w2_raw, 1, "w2_bf1"), "w2_1"))
-        for t in range(2, 4):
+        for t in range(1, 4):
             second_layer_tile(t)
 
-        def gather_op(window, offsets, other, op, name, out=None):
-            if out is None:
-                picked = sb.tile([P, 16 * offsets.shape[1]], F32, name=name, tag=name)
-                out = picked[:]
-            nc.vector.tensor_tensor(out, window[:].indirect(offsets[:]), other, op)
-            return out
+        def gather_op(out, window, offsets, other, op):
+            nc.vector.tensor_tensor(out, window[:].indirect(offsets), other, op)
 
-        res = sb.tile([P, 4, U], F32, name="res")
-        out_rows = out_0.rearrange("(p t) x -> p t x", t=4)
-        res_bf = sb.tile([P, U * PACK], BF16, name="res_bf", align_bytes=64)
-        z = {}
-
-        def round_pair(engine_copy, u):
-            engine_copy(
-                out=res_bf[:].rearrange("p (x t) -> p x t", t=4)[:, :, 2 * u : 2 * u + 2],
-                in_=res[:, 2 * u : 2 * u + 2, :].rearrange("p t x -> p x t"),
-            )
-
-        def add_on_tensor(terms, out, banks, name):
-            blocks = out.shape[1] // P
+        def add_on_tensor(terms, factor, banks, name):
+            width = terms[0].shape[1]
+            blocks = width // P
             turned = bank(banks[0], name + "_turned")
             for i, term in enumerate(terms):
                 for b in range(blocks):
@@ -218,39 +188,74 @@ def tile_picked_zappnp_gelu_po_kernel(
                         turned[:, P * b : P * (b + 1)], lhsT=term[:, P * b : P * (b + 1)], rhs=ident[:],
                         start=(i == 0 and b == 0), stop=(i == len(terms) - 1 and b == blocks - 1), is_transpose=True,
                     )
-            total = sb.tile([P, P * blocks], F32, name=name + "_total")
-            nc.scalar.copy(out=total[:], in_=turned[:, 0 : P * blocks])
+            total_t = sb.tile([P, width], F32, name=name + "_total_t", tag=name + "_total_t", align_bytes=64)
+            nc.scalar.copy(out=total_t[:], in_=turned[:, 0:width])
             back = bank(banks[1], name + "_back")
             for b in range(blocks):
-                nc.tensor.transpose(back[:, P * b : P * (b + 1)], total[:, P * b : P * (b + 1)], ident[:])
-            nc.scalar.copy(out=out, in_=back[:, 0 : P * blocks])
+                nc.tensor.transpose(back[:, P * b : P * (b + 1)], total_t[:, P * b : P * (b + 1)], ident[:])
+            total = sb.tile([P, width], F32, name=name + "_total", tag=name + "_total")
+            nc.scalar.activation(total[:], back[:, 0:width], COPY, scale=factor)
+            return total
 
-        def first_step(t):
-            a = gather_op(y[t], pos1_sb, gate_row[0][:], MULT, f"a{t}")
-            b = gather_op(y[t], pos2_sb, gate_row[1][:], MULT, f"b{t}")
-            c = sb.tile([P, V], F32, name=f"c{t}")
-            nc.vector.tensor_copy(c[:], y[t][:].indirect(cen_sb[:]))
-            z[t] = sb.tile([P, V], F32, name=f"z{t}")
-            pair = (5, 6) if t % 2 == 0 else (7, 0)
-            add_on_tensor([a, b, c[:]], z[t][:], pair if t < 2 else pair[::-1], f"z{t}")
+        def neighbours(terms, window, lists, gates):
+            for d in range(2):
+                gather_op(terms[d], window, lists[d][:], gates[d], MULT)
 
-        def second_step(t):
-            d = gather_op(z[t], nxt1_sb, gate2_row[0][:], MULT, "", out=late[t // 2][:, t % 2, :])
-            e = gather_op(z[t], nxt2_sb, gate2_row[1][:], MULT, "", out=late[2 + t // 2][:, t % 2, :])
-            both = sb.tile([P, U], F32, name=f"both{t}")
-            nc.vector.tensor_tensor(both[:], d, e, ADD)
-            gather_op(y[t], root_sb, both[:], ADD, "", out=res[:, t, :])
-            nc.sync.dma_start(out=out_rows[:, t, :], in_=res[:, t, :])
-
+        z = []
         for t in range(4):
-            first_step(t)
-        late = [sb.tile([P, 2, U], F32, name=f"late{i}", tag=tag) for i, tag in enumerate(["gate_row1", "gate_row0", "a3", "a2"])]
-        for t in range(4):
-            second_step(t)
+            near = sb.tile([P, 2, V], F32, name=f"near{t}")
+            terms = [near[:, d, :] for d in range(2)]
+            neighbours(terms, y[t], [pos1_sb, pos2_sb], [gate_row[0][:], gate_row[1][:]])
+            total = add_on_tensor(terms, 4.0, ((1, 2), (3, 4), (2, 1), (4, 3))[t], f"near{t}")
+            z_t = sb.tile([P, V], F32, name=f"z{t}")
+            gather_op(z_t[:], y[t], cen_sb[:], total[:], ADD)
+            z.append(z_t)
+
+        far0 = sb.tile([P, 2, U], F32, name="far0", tag="near2_total_t", align_bytes=64)
+        shared = sb.tile([P, 4, U], F32, name="shared", tag="near3_total_t", align_bytes=64)
+        far2 = sb.tile([P, 2, U], F32, name="far2", tag="far2")
+        far3 = sb.tile([P, 2, U], F32, name="far3")
+        nc.scalar.activation(shared[:, 2:4, :], gate2_raw[:], COPY, scale=0.8)
+        totals = {}
+        for t, far in enumerate((far0, shared, far2, far3)):
+            terms = [far[:, d, :] for d in range(2)]
+            gates = [gate2_raw[:, d, :] if t < 2 else shared[:, 2 + d, :] for d in range(2)]
+            neighbours(terms, z[t], [nxt1_sb, nxt2_sb], gates)
+            if t < 3:
+                totals[t] = add_on_tensor(terms, 0.8 if t < 2 else 1.0, ((4, 5), (6, 7), (0, 2))[t], f"next{t}")
+            else:
+                totals[t] = sb.tile([P, U], F32, name="next3_total")
+                nc.vector.tensor_tensor(totals[t][:], terms[0], terms[1], ADD)
+
+        res = [sb.tile([P, 2, U], F32, name=f"res{u}", tag=("far2", "res1")[u]) for u in range(2)]
+        out_rows = out_0.rearrange("(p t) x -> p t x", t=4)
+        res_bf = sb.tile([P, U * PACK], BF16, name="res_bf", tag="next2_total_t", align_bytes=64)
+
+        def round_pair(engine_copy, u, cols):
+            engine_copy(
+                out=res_bf[:].rearrange("p (x t) -> p x t", t=4)[:, cols, 2 * u : 2 * u + 2],
+                in_=res[u][:, :, cols].rearrange("p t x -> p x t"),
+            )
+
+        for t in (0, 1, 3):
+            gather_op(res[t // 2][:, t % 2, :], y[t], root_sb[:], totals[t][:], ADD)
+            nc.sync.dma_start(out=out_rows[:, t, :], in_=res[t // 2][:, t % 2, :])
             if t == 1:
-                round_pair(nc.scalar.copy, 0)
-        round_pair(nc.vector.tensor_copy, 1)
-        o_codes, o_scales = quantize(res_bf, "o")
+                round_pair(nc.scalar.copy, 0, slice(0, U))
+        halves = [slice(0, U // 2), slice(U // 2, U)]
+        for i, cols in enumerate(halves):
+            gather_op(res[1][:, 0, cols], y[2], root_sb[:, 8 * i : 8 * (i + 1)], totals[2][:, cols], ADD)
+        nc.sync.dma_start(out=out_rows[:, 2, :], in_=res[1][:, 0, :])
+        o_codes = sb.tile([P, U], U32, name="o_codes", align_bytes=64)
+        o_scales = sb.tile([P, U], U8, name="o_scales", align_bytes=64)
+        for cols in halves:
+            round_pair(nc.vector.tensor_copy, 1, cols)
+        for cols in halves:
+            nc.vector.quantize_mx(
+                out=o_codes[:, cols].bitcast(FP8X4),
+                scales=o_scales[:, cols],
+                in_=res_bf[:, PACK * cols.start : PACK * cols.stop],
+            )
         nc.sync.dma_start(out=out_1[0].rearrange("p n r -> p (n r)").bitcast(I32), in_=o_codes[:].bitcast(I32))
         for q in range(4):
             eng = nc.scalar if q % 2 == 0 else nc.sync

@@ -20,10 +20,14 @@ ADD = mybir.AluOpType.add
 
 P = 128
 PACK = 4
+K_PASS = P * PACK
 BANK = 512
-CHUNK = 128
-SLICE = 256
-H_BANKS = 8
+BANKS = 8
+GROUP = 16
+CHUNK = BANK // PACK
+SLICE = 2 * CHUNK
+RESTART = 0.2
+SPREAD = 0.8
 
 
 def tile_picked_zappnp_gelu_po_kernel(
@@ -34,8 +38,8 @@ def tile_picked_zappnp_gelu_po_kernel(
         sb = ctx.enter_context(tc.tile_pool(name="sb", bufs=1))
         psum = ctx.enter_context(tc.psum_pool(name="psum", bufs=1))
 
-        def bank(b, name):
-            return psum.tile([P, BANK], F32, name=name, tag=f"bank{b}")
+        def bank(index, name):
+            return psum.tile([P, BANK], F32, name=name, tag=f"bank{index}")
 
         def load_list(src, name):
             tile = sb.tile(list(src.shape), U16, name=name)
@@ -43,7 +47,7 @@ def tile_picked_zappnp_gelu_po_kernel(
             return tile
 
         def load_weight(rows, name):
-            raw = sb.tile([P, PACK, 512], F32, name=name)
+            raw = sb.tile([P, PACK, rows.shape[1]], F32, name=name)
             nc.sync.dma_start(out=raw[:], in_=rows.rearrange("(p j) c -> p j c", j=PACK))
             return raw
 
@@ -59,11 +63,10 @@ def tile_picked_zappnp_gelu_po_kernel(
                 out=xs_win[32 * q : 32 * q + 8, :].bitcast(I32), in_=x_scales[:, 4 * q : 4 * q + 4, :].bitcast(I32)
             )
         offs_sb = load_list(offs, "offs_sb")
-        pos1_sb = load_list(pos1, "pos1_sb")
-        pos2_sb = load_list(pos2, "pos2_sb")
-        w1_raw0 = load_weight(w1[0:512, :], "w1_raw0")
+        pos_sb = [load_list(pos1, "pos1_sb"), load_list(pos2, "pos2_sb")]
+        w1_raw0 = load_weight(w1[0:K_PASS, :], "w1_raw0")
         x_win0 = load_words(0)
-        w1_raw1 = load_weight(w1[512:1024, :], "w1_raw1")
+        w1_raw1 = load_weight(w1[K_PASS:K, :], "w1_raw1")
         x_win1 = load_words(1)
         w2_raw = load_weight(w2, "w2_raw")
         gate_row = []
@@ -72,18 +75,17 @@ def tile_picked_zappnp_gelu_po_kernel(
             nc.sync.dma_start(out=row[:], in_=gate[d])
             gate_row.append(row)
         cen_sb = load_list(cen, "cen_sb")
-        nxt1_sb = load_list(nxt1, "nxt1_sb")
-        nxt2_sb = load_list(nxt2, "nxt2_sb")
-        gate2_raw = sb.tile([P, 2, U], F32, name="gate2_raw")
-        nc.sync.dma_start(out=gate2_raw[:], in_=gate2.rearrange("d p x -> p d x"))
+        nxt_sb = [load_list(nxt1, "nxt1_sb"), load_list(nxt2, "nxt2_sb")]
+        gate2_row = sb.tile([P, 2, U], F32, name="gate2_row")
+        nc.sync.dma_start(out=gate2_row[:], in_=gate2.rearrange("d p x -> p d x"))
         root_sb = load_list(root, "root_sb")
 
         ident = sb.tile([P, P], F32, name="ident")
         make_identity(nc, ident[:])
 
-        def cast_pair(engine_copy, raw, u, name):
+        def round_weight(engine_copy, raw, u, name):
             grouped = sb.tile([P, 2 * P * PACK], BF16, name=name, align_bytes=64)
-            src = raw[:].rearrange("p j (m t) -> p m j t", t=4)[:, :, :, 2 * u : 2 * u + 2]
+            src = raw[:].rearrange("p j (m t) -> p m j t", t=PACK)[:, :, :, 2 * u : 2 * u + 2]
             dst = grouped[:].rearrange("p (t m j) -> p m j t", t=2, j=PACK)
             engine_copy(out=dst, in_=src)
             return grouped
@@ -100,165 +102,173 @@ def tile_picked_zappnp_gelu_po_kernel(
             cols = slice(P * (t % 2), P * (t % 2 + 1))
             return dict(lhsT=codes[:, cols].bitcast(FP8X4), lhsT_scale=scales[:, cols])
 
+        def quantize_w1_pass(raw, g):
+            halves = [
+                round_weight(engine_copy, raw, u, f"w1_bf{g}{u}")
+                for u, engine_copy in enumerate((nc.vector.tensor_copy, nc.scalar.copy))
+            ]
+            return [quantize(half, f"w1_{g}{u}") for u, half in enumerate(halves)]
+
         xs = sb.tile([P, S], U8, name="xs", align_bytes=64)
         xg = [sb.tile([P, S], U32, name=f"xg{g}", align_bytes=64) for g in range(2)]
 
-        def gather_words(g, win, s):
-            nc.vector.tensor_copy(
-                xg[g][:, SLICE * s : SLICE * (s + 1)], win[:].bitcast(U32).indirect(offs_sb[:, 16 * s : 16 * (s + 1)])
-            )
+        def gather_words(g, win):
+            for s in range(0, S, SLICE):
+                entries = offs_sb[:, s // GROUP : (s + SLICE) // GROUP]
+                nc.vector.tensor_copy(xg[g][:, s : s + SLICE], win[:].bitcast(U32).indirect(entries))
 
         nc.vector.tensor_copy(xs[:], xs_win[:].indirect(offs_sb[:]))
-        w1_bf0 = [cast_pair(nc.vector.tensor_copy, w1_raw0, 0, "w1_bf00"), cast_pair(nc.scalar.copy, w1_raw0, 1, "w1_bf01")]
-        w1_q0 = [quantize(w1_bf0[u], f"w1_0{u}") for u in range(2)]
-        for s in range(S // SLICE):
-            gather_words(0, x_win0, s)
-
-        h_ps = {}
-
-        def layer1(g, wq, c):
-            cols = slice(CHUNK * c, CHUNK * (c + 1))
-            for t in range(4):
-                nc.tensor.matmul_mx(
-                    out=h_ps[c][:, CHUNK * t : CHUNK * (t + 1)],
-                    rhs=xg[g][:, cols].bitcast(FP8X4),
-                    rhs_scale=xs[4 * g : P, cols],
-                    start=(g == 0 and t == 0),
-                    stop=(g == 1 and t == 3),
-                    **stationary(wq, t),
-                )
-
-        w1_bf1 = [cast_pair(nc.vector.tensor_copy, w1_raw1, 0, "w1_bf10"), cast_pair(nc.scalar.copy, w1_raw1, 1, "w1_bf11")]
-        w1_q1 = [quantize(w1_bf1[u], f"w1_1{u}") for u in range(2)]
-        for s in range(S // SLICE):
-            gather_words(1, x_win1, s)
+        w1_q = [quantize_w1_pass(w1_raw0, 0)]
+        gather_words(0, x_win0)
+        w1_q.append(quantize_w1_pass(w1_raw1, 1))
+        gather_words(1, x_win1)
 
         h_bf = []
         for c in range(S // CHUNK):
-            h_ps[c] = bank(c % H_BANKS, f"h_ps{c}")
-            layer1(0, w1_q0, c)
-            layer1(1, w1_q1, c)
-            hb = sb.tile([P, CHUNK * PACK], BF16, name=f"h_bf{c}", align_bytes=64)
+            h_ps = bank(c, f"h_ps{c}")
+            cols = slice(CHUNK * c, CHUNK * (c + 1))
+            for g in range(2):
+                for t in range(PACK):
+                    nc.tensor.matmul_mx(
+                        out=h_ps[:, CHUNK * t : CHUNK * (t + 1)],
+                        rhs=xg[g][:, cols].bitcast(FP8X4),
+                        rhs_scale=xs[4 * g : P, cols],
+                        start=(g == 0 and t == 0),
+                        stop=(g == 1 and t == PACK - 1),
+                        **stationary(w1_q[g], t),
+                    )
+            chunk_bf = sb.tile([P, CHUNK * PACK], BF16, name=f"h_bf{c}", align_bytes=64)
             nc.scalar.activation(
-                hb[:].rearrange("p (n t) -> p n t", t=4), h_ps[c][:].rearrange("p (t n) -> p n t", t=4), GELU
+                chunk_bf[:].rearrange("p (n t) -> p n t", t=PACK), h_ps[:].rearrange("p (t n) -> p n t", t=PACK), GELU
             )
-            h_bf.append(hb)
+            h_bf.append(chunk_bf)
 
-        w2_q = [quantize(cast_pair(nc.vector.tensor_copy, w2_raw, 0, "w2_bf0"), "w2_0")]
-
+        w2_q = [quantize(round_weight(nc.vector.tensor_copy, w2_raw, 0, "w2_bf0"), "w2_0")]
         h_codes = sb.tile([P, S], U32, name="h_codes", align_bytes=64)
         h_scales = sb.tile([P, S], U8, name="h_scales", align_bytes=64)
-        y = [sb.tile([P, S], F32, name=f"y{t}") for t in range(4)]
+        y = [sb.tile([P, S], F32, name=f"y{t}") for t in range(PACK)]
 
         def layer2(t, acc, cols):
             nc.tensor.matmul_mx(
-                out=acc, rhs=h_codes[:, cols].bitcast(FP8X4), rhs_scale=h_scales[:, cols],
-                start=True, stop=True, **stationary(w2_q, t),
+                out=acc,
+                rhs=h_codes[:, cols].bitcast(FP8X4),
+                rhs_scale=h_scales[:, cols],
+                start=True,
+                stop=True,
+                **stationary(w2_q, t),
             )
 
-        for b, (c0, c1) in enumerate([(0, 4), (4, 7), (7, 8)]):
-            acc = bank(b, f"y0_ps{b}")
+        last_chunk = S // CHUNK - 1
+        for part, (c0, c1) in enumerate([(0, PACK), (PACK, last_chunk), (last_chunk, last_chunk + 1)]):
+            acc = bank(part, f"y0_ps{part}")
             for c in range(c0, c1):
                 cols = slice(CHUNK * c, CHUNK * (c + 1))
                 nc.vector.quantize_mx(out=h_codes[:, cols].bitcast(FP8X4), scales=h_scales[:, cols], in_=h_bf[c][:])
                 layer2(0, acc[:, CHUNK * (c - c0) : CHUNK * (c - c0 + 1)], cols)
-            nc.vector.tensor_scalar_mul(y[0][:, CHUNK * c0 : CHUNK * c1], acc[:, 0 : CHUNK * (c1 - c0)], 0.2)
+            nc.vector.tensor_scalar_mul(y[0][:, CHUNK * c0 : CHUNK * c1], acc[:, 0 : CHUNK * (c1 - c0)], RESTART)
 
-        def second_layer_tile(t):
+        w2_q.append(quantize(round_weight(nc.scalar.copy, w2_raw, 1, "w2_bf1"), "w2_1"))
+        for t in range(1, PACK):
             for half in range(2):
                 cols = slice(BANK * half, BANK * (half + 1))
-                acc = bank((2 * t + 1 + half) % 8, f"y{t}_ps{half}")
+                acc = bank((2 * t + 1 + half) % BANKS, f"y{t}_ps{half}")
                 layer2(t, acc[:], cols)
-                nc.scalar.activation(y[t][:, cols], acc[:], COPY, scale=0.2)
-
-        w2_q.append(quantize(cast_pair(nc.scalar.copy, w2_raw, 1, "w2_bf1"), "w2_1"))
-        for t in range(1, 4):
-            second_layer_tile(t)
+                nc.scalar.activation(y[t][:, cols], acc[:], COPY, scale=RESTART)
 
         def gather_op(out, window, offsets, other, op):
             nc.vector.tensor_tensor(out, window[:].indirect(offsets), other, op)
 
-        def add_on_tensor(terms, factor, banks, name):
-            width = terms[0].shape[1]
-            blocks = width // P
-            turned = bank(banks[0], name + "_turned")
-            for i, term in enumerate(terms):
-                for b in range(blocks):
-                    nc.tensor.matmul(
-                        turned[:, P * b : P * (b + 1)], lhsT=term[:, P * b : P * (b + 1)], rhs=ident[:],
-                        start=(i == 0 and b == 0), stop=(i == len(terms) - 1 and b == blocks - 1), is_transpose=True,
-                    )
-            total_t = sb.tile([P, width], F32, name=name + "_total_t", tag=name + "_total_t", align_bytes=64)
-            nc.scalar.copy(out=total_t[:], in_=turned[:, 0:width])
-            back = bank(banks[1], name + "_back")
-            for b in range(blocks):
-                nc.tensor.transpose(back[:, P * b : P * (b + 1)], total_t[:, P * b : P * (b + 1)], ident[:])
-            total = sb.tile([P, width], F32, name=name + "_total", tag=name + "_total")
-            nc.scalar.activation(total[:], back[:, 0:width], COPY, scale=factor)
-            return total
-
-        def neighbours(terms, window, lists, gates):
+        def gated_terms(terms, window, lists, gates):
             for d in range(2):
                 gather_op(terms[d], window, lists[d][:], gates[d], MULT)
 
+        def add_on_tensor(terms, factor, banks, name):
+            width = terms[0].shape[1]
+            squares = [slice(col, col + P) for col in range(0, width, P)]
+            sum_ps = bank(banks[0], name + "_sum_ps")
+            for i, term in enumerate(terms):
+                for cols in squares:
+                    nc.tensor.matmul(
+                        sum_ps[:, cols],
+                        lhsT=term[:, cols],
+                        rhs=ident[:],
+                        start=(i == 0 and cols.start == 0),
+                        stop=(i == len(terms) - 1 and cols.stop == width),
+                        is_transpose=True,
+                    )
+            turned = sb.tile([P, width], F32, name=name + "_turned", tag=name + "_turned", align_bytes=64)
+            nc.scalar.copy(out=turned[:], in_=sum_ps[:, 0:width])
+            back_ps = bank(banks[1], name + "_back_ps")
+            for cols in squares:
+                nc.tensor.transpose(back_ps[:, cols], turned[:, cols], ident[:])
+            total = sb.tile([P, width], F32, name=name + "_total")
+            nc.scalar.activation(total[:], back_ps[:, 0:width], COPY, scale=factor)
+            return total
+
         z = []
-        for t in range(4):
+        for t in range(PACK):
             near = sb.tile([P, 2, V], F32, name=f"near{t}")
             terms = [near[:, d, :] for d in range(2)]
-            neighbours(terms, y[t], [pos1_sb, pos2_sb], [gate_row[0][:], gate_row[1][:]])
-            total = add_on_tensor(terms, 4.0, ((1, 2), (3, 4), (2, 1), (4, 3))[t], f"near{t}")
+            gated_terms(terms, y[t], pos_sb, [gate_row[d][:] for d in range(2)])
+            pair = (1, 2) if t % 2 == 0 else (3, 4)
+            total = add_on_tensor(terms, SPREAD / RESTART, pair if t < 2 else pair[::-1], f"near{t}")
             z_t = sb.tile([P, V], F32, name=f"z{t}")
             gather_op(z_t[:], y[t], cen_sb[:], total[:], ADD)
             z.append(z_t)
 
-        far0 = sb.tile([P, 2, U], F32, name="far0", tag="near2_total_t", align_bytes=64)
-        shared = sb.tile([P, 4, U], F32, name="shared", tag="near3_total_t", align_bytes=64)
+        far0 = sb.tile([P, 2, U], F32, name="far0", tag="near2_turned", align_bytes=64)
+        far1_and_gates = sb.tile([P, 4, U], F32, name="far1_and_gates", tag="near3_turned", align_bytes=64)
         far2 = sb.tile([P, 2, U], F32, name="far2", tag="far2")
         far3 = sb.tile([P, 2, U], F32, name="far3")
-        nc.scalar.activation(shared[:, 2:4, :], gate2_raw[:], COPY, scale=0.8)
-        totals = {}
-        for t, far in enumerate((far0, shared, far2, far3)):
+        nc.scalar.activation(far1_and_gates[:, 2:4, :], gate2_row[:], COPY, scale=SPREAD)
+        far_banks = ((4, 5), (6, 7), (0, 2))
+        far_total = []
+        for t, far in enumerate((far0, far1_and_gates, far2, far3)):
             terms = [far[:, d, :] for d in range(2)]
-            gates = [gate2_raw[:, d, :] if t < 2 else shared[:, 2 + d, :] for d in range(2)]
-            neighbours(terms, z[t], [nxt1_sb, nxt2_sb], gates)
-            if t < 3:
-                totals[t] = add_on_tensor(terms, 0.8 if t < 2 else 1.0, ((4, 5), (6, 7), (0, 2))[t], f"next{t}")
+            scaled = t >= 2
+            gates = [far1_and_gates[:, 2 + d, :] if scaled else gate2_row[:, d, :] for d in range(2)]
+            gated_terms(terms, z[t], nxt_sb, gates)
+            if t < PACK - 1:
+                far_total.append(add_on_tensor(terms, 1.0 if scaled else SPREAD, far_banks[t], f"far{t}"))
             else:
-                totals[t] = sb.tile([P, U], F32, name="next3_total")
-                nc.vector.tensor_tensor(totals[t][:], terms[0], terms[1], ADD)
+                total = sb.tile([P, U], F32, name="far3_total")
+                nc.vector.tensor_tensor(total[:], terms[0], terms[1], ADD)
+                far_total.append(total)
 
-        res = [sb.tile([P, 2, U], F32, name=f"res{u}", tag=("far2", "res1")[u]) for u in range(2)]
-        out_rows = out_0.rearrange("(p t) x -> p t x", t=4)
-        res_bf = sb.tile([P, U * PACK], BF16, name="res_bf", tag="next2_total_t", align_bytes=64)
+        res = [sb.tile([P, 2, U], F32, name="res0", tag="far2"), sb.tile([P, 2, U], F32, name="res1")]
+        out_rows = out_0.rearrange("(p t) x -> p t x", t=PACK)
+        res_bf = sb.tile([P, U * PACK], BF16, name="res_bf", tag="far2_turned", align_bytes=64)
 
-        def round_pair(engine_copy, u, cols):
+        def round_result(engine_copy, u, cols):
             engine_copy(
-                out=res_bf[:].rearrange("p (x t) -> p x t", t=4)[:, cols, 2 * u : 2 * u + 2],
+                out=res_bf[:].rearrange("p (x t) -> p x t", t=PACK)[:, cols, 2 * u : 2 * u + 2],
                 in_=res[u][:, :, cols].rearrange("p t x -> p x t"),
             )
 
         for t in (0, 1, 3):
-            gather_op(res[t // 2][:, t % 2, :], y[t], root_sb[:], totals[t][:], ADD)
+            gather_op(res[t // 2][:, t % 2, :], y[t], root_sb[:], far_total[t][:], ADD)
             nc.sync.dma_start(out=out_rows[:, t, :], in_=res[t // 2][:, t % 2, :])
             if t == 1:
-                round_pair(nc.scalar.copy, 0, slice(0, U))
-        halves = [slice(0, U // 2), slice(U // 2, U)]
-        for i, cols in enumerate(halves):
-            gather_op(res[1][:, 0, cols], y[2], root_sb[:, 8 * i : 8 * (i + 1)], totals[2][:, cols], ADD)
+                round_result(nc.scalar.copy, 0, slice(0, U))
+        col_halves = [slice(0, U // 2), slice(U // 2, U)]
+        for cols in col_halves:
+            entries = root_sb[:, cols.start // GROUP : cols.stop // GROUP]
+            gather_op(res[1][:, 0, cols], y[2], entries, far_total[2][:, cols], ADD)
         nc.sync.dma_start(out=out_rows[:, 2, :], in_=res[1][:, 0, :])
         o_codes = sb.tile([P, U], U32, name="o_codes", align_bytes=64)
         o_scales = sb.tile([P, U], U8, name="o_scales", align_bytes=64)
-        for cols in halves:
-            round_pair(nc.vector.tensor_copy, 1, cols)
-        for cols in halves:
+        for cols in col_halves:
+            round_result(nc.vector.tensor_copy, 1, cols)
+        for cols in col_halves:
             nc.vector.quantize_mx(
                 out=o_codes[:, cols].bitcast(FP8X4),
                 scales=o_scales[:, cols],
                 in_=res_bf[:, PACK * cols.start : PACK * cols.stop],
             )
+
         nc.sync.dma_start(out=out_1[0].rearrange("p n r -> p (n r)").bitcast(I32), in_=o_codes[:].bitcast(I32))
         for q in range(4):
-            eng = nc.scalar if q % 2 == 0 else nc.sync
-            eng.dma_start(
+            queue = nc.scalar if q % 2 == 0 else nc.sync
+            queue.dma_start(
                 out=out_2[0, 4 * q : 4 * q + 4, :].bitcast(I32), in_=o_scales[32 * q : 32 * q + 4, :].bitcast(I32)
             )

@@ -51,27 +51,28 @@ def tile_picked_zappnp_gelu_po_kernel(
             nc.sync.dma_start(out=raw[:], in_=rows.rearrange("(p j) c -> p j c", j=PACK))
             return raw
 
-        def load_words(g):
-            tile = sb.tile([P, T], I32, name=f"x_win{g}")
-            nc.sync.dma_start(out=tile[:], in_=x_words[g].rearrange("p n r -> p (n r)").bitcast(I32))
-            return tile
+        def load_words(tile, g, cols):
+            nc.sync.dma_start(out=tile[:, cols], in_=x_words[g].rearrange("p n r -> p (n r)").bitcast(I32)[:, cols])
 
         xs_win = sb.tile([P, T], U8, name="xs_win")
         nc.gpsimd.memset(xs_win[:].bitcast(I32), 0)
+        x_win0 = sb.tile([P, T], I32, name="x_win0")
+        load_words(x_win0, 0, slice(0, T // 4))
+        offs_sb = load_list(offs, "offs_sb")
         for q in range(4):
             nc.sync.dma_start(
                 out=xs_win[32 * q : 32 * q + 8, :].bitcast(I32), in_=x_scales[:, 4 * q : 4 * q + 4, :].bitcast(I32)
             )
-        offs_sb = load_list(offs, "offs_sb")
-        pos_sb = [load_list(pos1, "pos1_sb"), load_list(pos2, "pos2_sb")]
         w1_raw0 = load_weight(w1[0:K_PASS, :], "w1_raw0")
-        x_win0 = load_words(0)
+        load_words(x_win0, 0, slice(T // 4, T))
         w1_raw1 = load_weight(w1[K_PASS:K, :], "w1_raw1")
-        x_win1 = load_words(1)
+        x_win1 = sb.tile([P, T], I32, name="x_win1")
+        load_words(x_win1, 1, slice(0, T))
         w2_raw = load_weight(w2, "w2_raw")
+        pos_sb = [load_list(pos1, "pos1_sb"), load_list(pos2, "pos2_sb")]
         gate_row = []
         for d in range(2):
-            row = sb.tile([P, V], F32, name=f"gate_row{d}")
+            row = sb.tile([P, V], F32, name=f"gate_row{d}", tag=f"gate_row{d}")
             nc.sync.dma_start(out=row[:], in_=gate[d])
             gate_row.append(row)
         cen_sb = load_list(cen, "cen_sb")
@@ -159,19 +160,25 @@ def tile_picked_zappnp_gelu_po_kernel(
             )
 
         last_chunk = S // CHUNK - 1
-        for part, (c0, c1) in enumerate([(0, PACK), (PACK, last_chunk), (last_chunk, last_chunk + 1)]):
+        parts = [(0, PACK), (PACK, last_chunk - 1), (last_chunk - 1, last_chunk), (last_chunk, last_chunk + 1)]
+        for part, (c0, c1) in enumerate(parts):
             acc = bank(part, f"y0_ps{part}")
             for c in range(c0, c1):
                 cols = slice(CHUNK * c, CHUNK * (c + 1))
                 nc.vector.quantize_mx(out=h_codes[:, cols].bitcast(FP8X4), scales=h_scales[:, cols], in_=h_bf[c][:])
                 layer2(0, acc[:, CHUNK * (c - c0) : CHUNK * (c - c0 + 1)], cols)
-            nc.vector.tensor_scalar_mul(y[0][:, CHUNK * c0 : CHUNK * c1], acc[:, 0 : CHUNK * (c1 - c0)], RESTART)
+            if part != 1:
+                nc.vector.tensor_scalar_mul(y[0][:, CHUNK * c0 : CHUNK * c1], acc[:, 0 : CHUNK * (c1 - c0)], RESTART)
+            else:
+                nc.scalar.activation(
+                    y[0][:, CHUNK * c0 : CHUNK * c1], acc[:, 0 : CHUNK * (c1 - c0)], COPY, scale=RESTART
+                )
 
-        w2_q.append(quantize(round_weight(nc.scalar.copy, w2_raw, 1, "w2_bf1"), "w2_1"))
+        w2_q.append(quantize(round_weight(nc.vector.tensor_copy, w2_raw, 1, "w2_bf1"), "w2_1"))
         for t in range(1, PACK):
             for half in range(2):
                 cols = slice(BANK * half, BANK * (half + 1))
-                acc = bank((2 * t + 1 + half) % BANKS, f"y{t}_ps{half}")
+                acc = bank((2 * t + 2 + half) % BANKS, f"y{t}_ps{half}")
                 layer2(t, acc[:], cols)
                 nc.scalar.activation(y[t][:, cols], acc[:], COPY, scale=RESTART)
 
@@ -210,9 +217,9 @@ def tile_picked_zappnp_gelu_po_kernel(
             near = sb.tile([P, 2, V], F32, name=f"near{t}")
             terms = [near[:, d, :] for d in range(2)]
             gated_terms(terms, y[t], pos_sb, [gate_row[d][:] for d in range(2)])
-            pair = (1, 2) if t % 2 == 0 else (3, 4)
+            pair = (2, 3) if t % 2 == 0 else (4, 5)
             total = add_on_tensor(terms, SPREAD / RESTART, pair if t < 2 else pair[::-1], f"near{t}")
-            z_t = sb.tile([P, V], F32, name=f"z{t}")
+            z_t = sb.tile([P, V], F32, name=f"z{t}", tag="gate_row0" if t == 0 else f"z{t}")
             gather_op(z_t[:], y[t], cen_sb[:], total[:], ADD)
             z.append(z_t)
 
@@ -221,7 +228,7 @@ def tile_picked_zappnp_gelu_po_kernel(
         far2 = sb.tile([P, 2, U], F32, name="far2", tag="far2")
         far3 = sb.tile([P, 2, U], F32, name="far3")
         nc.scalar.activation(far1_and_gates[:, 2:4, :], gate2_row[:], COPY, scale=SPREAD)
-        far_banks = ((4, 5), (6, 7), (0, 2))
+        far_banks = ((5, 6), (7, 0), (1, 3))
         far_total = []
         for t, far in enumerate((far0, far1_and_gates, far2, far3)):
             terms = [far[:, d, :] for d in range(2)]

@@ -103,10 +103,10 @@ def tile_picked_zappnp_gelu_po_kernel(
             cols = slice(P * (t % 2), P * (t % 2 + 1))
             return dict(lhsT=codes[:, cols].bitcast(FP8X4), lhsT_scale=scales[:, cols])
 
-        def quantize_w1_pass(raw, g):
+        def quantize_w1_pass(raw, g, copies):
             halves = [
                 round_weight(engine_copy, raw, u, f"w1_bf{g}{u}")
-                for u, engine_copy in enumerate((nc.vector.tensor_copy, nc.scalar.copy))
+                for u, engine_copy in enumerate(copies)
             ]
             return [quantize(half, f"w1_{g}{u}") for u, half in enumerate(halves)]
 
@@ -119,9 +119,9 @@ def tile_picked_zappnp_gelu_po_kernel(
                 nc.vector.tensor_copy(xg[g][:, s : s + SLICE], win[:].bitcast(U32).indirect(entries))
 
         nc.vector.tensor_copy(xs[:], xs_win[:].indirect(offs_sb[:]))
-        w1_q = [quantize_w1_pass(w1_raw0, 0)]
+        w1_q = [quantize_w1_pass(w1_raw0, 0, (nc.vector.tensor_copy, nc.scalar.copy))]
         gather_words(0, x_win0)
-        w1_q.append(quantize_w1_pass(w1_raw1, 1))
+        w1_q.append(quantize_w1_pass(w1_raw1, 1, (nc.vector.tensor_copy, nc.scalar.copy)))
         gather_words(1, x_win1)
 
         h_bf = []
@@ -160,21 +160,16 @@ def tile_picked_zappnp_gelu_po_kernel(
             )
 
         last_chunk = S // CHUNK - 1
-        parts = [(0, PACK), (PACK, last_chunk - 1), (last_chunk - 1, last_chunk), (last_chunk, last_chunk + 1)]
+        parts = [(0, PACK), (PACK, last_chunk), (last_chunk, last_chunk + 1)]
         for part, (c0, c1) in enumerate(parts):
             acc = bank(part, f"y0_ps{part}")
             for c in range(c0, c1):
                 cols = slice(CHUNK * c, CHUNK * (c + 1))
                 nc.vector.quantize_mx(out=h_codes[:, cols].bitcast(FP8X4), scales=h_scales[:, cols], in_=h_bf[c][:])
                 layer2(0, acc[:, CHUNK * (c - c0) : CHUNK * (c - c0 + 1)], cols)
-            if part != 1:
-                nc.vector.tensor_scalar_mul(y[0][:, CHUNK * c0 : CHUNK * c1], acc[:, 0 : CHUNK * (c1 - c0)], RESTART)
-            else:
-                nc.scalar.activation(
-                    y[0][:, CHUNK * c0 : CHUNK * c1], acc[:, 0 : CHUNK * (c1 - c0)], COPY, scale=RESTART
-                )
+            nc.vector.tensor_scalar_mul(y[0][:, CHUNK * c0 : CHUNK * c1], acc[:, 0 : CHUNK * (c1 - c0)], RESTART)
 
-        w2_q.append(quantize(round_weight(nc.vector.tensor_copy, w2_raw, 1, "w2_bf1"), "w2_1"))
+        w2_q.append(quantize(round_weight(nc.scalar.copy, w2_raw, 1, "w2_bf1"), "w2_1"))
         for t in range(1, PACK):
             for half in range(2):
                 cols = slice(BANK * half, BANK * (half + 1))

@@ -26,6 +26,7 @@ BANKS = 8
 GROUP = 16
 CHUNK = BANK // PACK
 SLICE = 2 * CHUNK
+Y0_PARTS = 3
 RESTART = 0.2
 SPREAD = 0.8
 
@@ -59,15 +60,30 @@ def tile_picked_zappnp_gelu_po_kernel(
         x_win0 = sb.tile([P, T], I32, name="x_win0")
         load_words(x_win0, 0, slice(0, T // 4))
         offs_sb = load_list(offs, "offs_sb")
-        for q in range(4):
-            nc.sync.dma_start(
-                out=xs_win[32 * q : 32 * q + 8, :].bitcast(I32), in_=x_scales[:, 4 * q : 4 * q + 4, :].bitcast(I32)
-            )
+        nc.sync.dma_start(
+            out=xs_win[0:P:4, :].bitcast(I32), in_=x_scales.rearrange("g r c -> (g r) c").bitcast(I32)
+        )
         w1_raw0 = load_weight(w1[0:K_PASS, :], "w1_raw0")
         load_words(x_win0, 0, slice(T // 4, T))
         w1_raw1 = load_weight(w1[K_PASS:K, :], "w1_raw1")
+
+        xs_picked = sb.tile([P, S], U8, name="xs_picked")
+        nc.vector.tensor_copy(xs_picked[:], xs_win[:].indirect(offs_sb[:]))
+
+        def place_scales(g):
+            plane = sb.tile([P, S], U8, name=f"xs{g}", align_bytes=64)
+            nc.gpsimd.memset(plane[:].bitcast(I32), 0)
+            for q in range(4):
+                first = 4 * (16 * g + 4 * q)
+                nc.sync.dma_start(
+                    out=plane[32 * q : 32 * q + 4, :].bitcast(I32), in_=xs_picked[first : first + 16 : 4, :].bitcast(I32)
+                )
+            return plane
+
+        xs = [place_scales(0)]
         x_win1 = sb.tile([P, T], I32, name="x_win1")
         load_words(x_win1, 1, slice(0, T))
+        xs.append(place_scales(1))
         w2_raw = load_weight(w2, "w2_raw")
         pos_sb = [load_list(pos1, "pos1_sb"), load_list(pos2, "pos2_sb")]
         gate_row = []
@@ -110,7 +126,6 @@ def tile_picked_zappnp_gelu_po_kernel(
             ]
             return [quantize(half, f"w1_{g}{u}") for u, half in enumerate(halves)]
 
-        xs = sb.tile([P, S], U8, name="xs", align_bytes=64)
         xg = [sb.tile([P, S], U32, name=f"xg{g}", align_bytes=64) for g in range(2)]
 
         def gather_words(g, win):
@@ -118,7 +133,6 @@ def tile_picked_zappnp_gelu_po_kernel(
                 entries = offs_sb[:, s // GROUP : (s + SLICE) // GROUP]
                 nc.vector.tensor_copy(xg[g][:, s : s + SLICE], win[:].bitcast(U32).indirect(entries))
 
-        nc.vector.tensor_copy(xs[:], xs_win[:].indirect(offs_sb[:]))
         w1_q = [quantize_w1_pass(w1_raw0, 0, (nc.vector.tensor_copy, nc.scalar.copy))]
         gather_words(0, x_win0)
         w1_q.append(quantize_w1_pass(w1_raw1, 1, (nc.vector.tensor_copy, nc.scalar.copy)))
@@ -126,14 +140,14 @@ def tile_picked_zappnp_gelu_po_kernel(
 
         h_bf = []
         for c in range(S // CHUNK):
-            h_ps = bank(c, f"h_ps{c}")
+            h_ps = bank(Y0_PARTS + c % (BANKS - Y0_PARTS), f"h_ps{c}")
             cols = slice(CHUNK * c, CHUNK * (c + 1))
             for g in range(2):
                 for t in range(PACK):
                     nc.tensor.matmul_mx(
                         out=h_ps[:, CHUNK * t : CHUNK * (t + 1)],
                         rhs=xg[g][:, cols].bitcast(FP8X4),
-                        rhs_scale=xs[4 * g : P, cols],
+                        rhs_scale=xs[g][:, cols],
                         start=(g == 0 and t == 0),
                         stop=(g == 1 and t == PACK - 1),
                         **stationary(w1_q[g], t),

@@ -72,7 +72,7 @@ def tile_picked_zappnp_gelu_po_kernel(
 
         def place_scales(g):
             plane = sb.tile([P, S], U8, name=f"xs{g}", align_bytes=64)
-            nc.gpsimd.memset(plane[:].bitcast(I32), 0)
+            nc.vector.memset(plane[:].bitcast(I32), 0)
             for q in range(4):
                 first = 4 * (16 * g + 4 * q)
                 nc.sync.dma_start(
@@ -100,16 +100,17 @@ def tile_picked_zappnp_gelu_po_kernel(
         ident = sb.tile([P, P], F32, name="ident")
         make_identity(nc, ident[:])
 
-        def round_weight(engine_copy, raw, u, name):
+        def round_weight(shares, raw, u, name):
             grouped = sb.tile([P, 2 * P * PACK], BF16, name=name, align_bytes=64)
             src = raw[:].rearrange("p j (m t) -> p m j t", t=PACK)[:, :, :, 2 * u : 2 * u + 2]
             dst = grouped[:].rearrange("p (t m j) -> p m j t", t=2, j=PACK)
-            engine_copy(out=dst, in_=src)
+            for engine_copy, cols in shares:
+                engine_copy(out=dst[:, cols], in_=src[:, cols])
             return grouped
 
-        def quantize(grouped, name):
+        def quantize(grouped, name, tag=None):
             width = grouped.shape[1] // PACK
-            codes = sb.tile([P, width], U32, name=name + "_codes", align_bytes=64)
+            codes = sb.tile([P, width], U32, name=name + "_codes", tag=tag or name + "_codes", align_bytes=64)
             scales = sb.tile([P, width], U8, name=name + "_scales", align_bytes=64)
             nc.vector.quantize_mx(out=codes[:].bitcast(FP8X4), scales=scales[:], in_=grouped[:])
             return codes, scales
@@ -119,26 +120,27 @@ def tile_picked_zappnp_gelu_po_kernel(
             cols = slice(P * (t % 2), P * (t % 2 + 1))
             return dict(lhsT=codes[:, cols].bitcast(FP8X4), lhsT_scale=scales[:, cols])
 
-        def quantize_w1_pass(raw, g, copies):
-            halves = [
-                round_weight(engine_copy, raw, u, f"w1_bf{g}{u}")
-                for u, engine_copy in enumerate(copies)
-            ]
+        on_vector = [(nc.vector.tensor_copy, slice(0, P))]
+        shared = [(nc.vector.tensor_copy, slice(0, P // 4)), (nc.scalar.copy, slice(P // 4, P))]
+
+        def quantize_w1_pass(raw, g, shares):
+            halves = [round_weight(shares[u], raw, u, f"w1_bf{g}{u}") for u in range(2)]
             return [quantize(half, f"w1_{g}{u}") for u, half in enumerate(halves)]
 
         xg = [sb.tile([P, S], U32, name=f"xg{g}", align_bytes=64) for g in range(2)]
 
-        def gather_words(g, win):
-            for s in range(0, S, SLICE):
-                entries = offs_sb[:, s // GROUP : (s + SLICE) // GROUP]
-                nc.vector.tensor_copy(xg[g][:, s : s + SLICE], win[:].bitcast(U32).indirect(entries))
+        def gather_words(g, win, cuts):
+            for s0, s1 in zip(cuts, cuts[1:]):
+                entries = offs_sb[:, s0 // GROUP : s1 // GROUP]
+                nc.vector.tensor_copy(xg[g][:, s0:s1], win[:].bitcast(U32).indirect(entries))
 
-        w1_q = [quantize_w1_pass(w1_raw0, 0, (nc.vector.tensor_copy, nc.scalar.copy))]
-        gather_words(0, x_win0)
-        w1_q.append(quantize_w1_pass(w1_raw1, 1, (nc.vector.tensor_copy, nc.scalar.copy)))
-        gather_words(1, x_win1)
+        w1_q = [quantize_w1_pass(w1_raw0, 0, (on_vector, on_vector))]
+        gather_words(0, x_win0, [0, S // 2, S])
+        w1_q.append(quantize_w1_pass(w1_raw1, 1, (on_vector, shared)))
+        gather_words(1, x_win1, [0, SLICE, 2 * SLICE, S])
 
-        h_bf = []
+        h_groups = [(0, 2), (2, 4), (4, 6), (6, 7), (7, 8)]
+        h_bf = {}
         for c in range(S // CHUNK):
             h_ps = bank(Y0_PARTS + c % (BANKS - Y0_PARTS), f"h_ps{c}")
             cols = slice(CHUNK * c, CHUNK * (c + 1))
@@ -152,13 +154,17 @@ def tile_picked_zappnp_gelu_po_kernel(
                         stop=(g == 1 and t == PACK - 1),
                         **stationary(w1_q[g], t),
                     )
-            chunk_bf = sb.tile([P, CHUNK * PACK], BF16, name=f"h_bf{c}", align_bytes=64)
+            c0, c1 = next_group = [group for group in h_groups if group[0] <= c < group[1]][0]
+            if c == c0:
+                h_bf[next_group] = sb.tile(
+                    [P, (c1 - c0) * CHUNK * PACK], BF16, name=f"h_bf{c0}", tag=f"h_bf{c0}", align_bytes=64
+                )
+            chunk_bf = h_bf[next_group][:, BANK * (c - c0) : BANK * (c - c0 + 1)]
             nc.scalar.activation(
-                chunk_bf[:].rearrange("p (n t) -> p n t", t=PACK), h_ps[:].rearrange("p (t n) -> p n t", t=PACK), GELU
+                chunk_bf.rearrange("p (n t) -> p n t", t=PACK), h_ps[:].rearrange("p (t n) -> p n t", t=PACK), GELU
             )
-            h_bf.append(chunk_bf)
 
-        w2_q = [quantize(round_weight(nc.vector.tensor_copy, w2_raw, 0, "w2_bf0"), "w2_0")]
+        w2_q = [quantize(round_weight(on_vector, w2_raw, 0, "w2_bf0"), "w2_0")]
         h_codes = sb.tile([P, S], U32, name="h_codes", align_bytes=64)
         h_scales = sb.tile([P, S], U8, name="h_scales", align_bytes=64)
         y = [sb.tile([P, S], F32, name=f"y{t}") for t in range(PACK)]
@@ -174,20 +180,26 @@ def tile_picked_zappnp_gelu_po_kernel(
             )
 
         last_chunk = S // CHUNK - 1
-        parts = [(0, PACK), (PACK, last_chunk), (last_chunk, last_chunk + 1)]
-        for part, (c0, c1) in enumerate(parts):
+        parts = [(0, 2), (2, 2 + PACK), (last_chunk, last_chunk + 1), (last_chunk - 1, last_chunk)]
+        for part, (c0, c1) in sorted(enumerate(parts), key=lambda entry: entry[1]):
             acc = bank(part, f"y0_ps{part}")
-            for c in range(c0, c1):
-                cols = slice(CHUNK * c, CHUNK * (c + 1))
-                nc.vector.quantize_mx(out=h_codes[:, cols].bitcast(FP8X4), scales=h_scales[:, cols], in_=h_bf[c][:])
-                layer2(0, acc[:, CHUNK * (c - c0) : CHUNK * (c - c0 + 1)], cols)
-            nc.vector.tensor_scalar_mul(y[0][:, CHUNK * c0 : CHUNK * c1], acc[:, 0 : CHUNK * (c1 - c0)], RESTART)
+            for g0, g1 in h_groups:
+                if c0 <= g0 < c1:
+                    cols = slice(CHUNK * g0, CHUNK * g1)
+                    nc.vector.quantize_mx(
+                        out=h_codes[:, cols].bitcast(FP8X4), scales=h_scales[:, cols], in_=h_bf[g0, g1][:]
+                    )
+                    layer2(0, acc[:, CHUNK * (g0 - c0) : CHUNK * (g1 - c0)], cols)
+            if part == 0:
+                nc.vector.tensor_scalar_mul(y[0][:, CHUNK * c0 : CHUNK * c1], acc[:, 0 : CHUNK * (c1 - c0)], RESTART)
+            else:
+                nc.scalar.activation(y[0][:, CHUNK * c0 : CHUNK * c1], acc[:, 0 : CHUNK * (c1 - c0)], COPY, scale=RESTART)
 
-        w2_q.append(quantize(round_weight(nc.scalar.copy, w2_raw, 1, "w2_bf1"), "w2_1"))
+        w2_q.append(quantize(round_weight(on_vector, w2_raw, 1, "w2_bf1"), "w2_1", f"h_bf{last_chunk}"))
         for t in range(1, PACK):
             for half in range(2):
                 cols = slice(BANK * half, BANK * (half + 1))
-                acc = bank((2 * t + 2 + half) % BANKS, f"y{t}_ps{half}")
+                acc = bank(2 if (t, half) == (1, 0) else (2 * t + 2 + half) % BANKS, f"y{t}_ps{half}")
                 layer2(t, acc[:], cols)
                 nc.scalar.activation(y[t][:, cols], acc[:], COPY, scale=RESTART)
 

@@ -25,8 +25,11 @@ BANK = 512
 BANKS = 8
 GROUP = 16
 CHUNK = BANK // PACK
+CHUNKS = S // CHUNK
 SLICE = 2 * CHUNK
-Y0_PARTS = 3
+H_BANK0 = 3
+SCALE_ROWS = 16
+ROW_STEP = P // (2 * SCALE_ROWS)
 RESTART = 0.2
 SPREAD = 0.8
 
@@ -58,27 +61,26 @@ def tile_picked_zappnp_gelu_po_kernel(
         xs_win = sb.tile([P, T], U8, name="xs_win")
         nc.gpsimd.memset(xs_win[:].bitcast(I32), 0)
         x_win0 = sb.tile([P, T], I32, name="x_win0")
-        load_words(x_win0, 0, slice(0, T // 4))
+        load_words(x_win0, 0, slice(0, 3 * T // 8))
         offs_sb = load_list(offs, "offs_sb")
         nc.sync.dma_start(
-            out=xs_win[0:P:4, :].bitcast(I32), in_=x_scales.rearrange("g r c -> (g r) c").bitcast(I32)
+            out=xs_win[0:P:ROW_STEP, :].bitcast(I32), in_=x_scales.rearrange("g r c -> (g r) c").bitcast(I32)
         )
         w1_raw0 = load_weight(w1[0:K_PASS, :], "w1_raw0")
-        load_words(x_win0, 0, slice(T // 4, T))
+        load_words(x_win0, 0, slice(3 * T // 8, T))
         w1_raw1 = load_weight(w1[K_PASS:K, :], "w1_raw1")
 
         xs_picked = sb.tile([P, S], U8, name="xs_picked")
         nc.vector.tensor_copy(xs_picked[:], xs_win[:].indirect(offs_sb[:]))
 
         def place_scales(g):
-            plane = sb.tile([P, S], U8, name=f"xs{g}", align_bytes=64)
-            nc.vector.memset(plane[:].bitcast(I32), 0)
+            scale_tile = sb.tile([P, S], U8, name=f"xs{g}", align_bytes=64)
+            nc.vector.memset(scale_tile[:].bitcast(I32), 0)
             for q in range(4):
-                first = 4 * (16 * g + 4 * q)
-                nc.sync.dma_start(
-                    out=plane[32 * q : 32 * q + 4, :].bitcast(I32), in_=xs_picked[first : first + 16 : 4, :].bitcast(I32)
-                )
-            return plane
+                first = ROW_STEP * (SCALE_ROWS * g + 4 * q)
+                rows = xs_picked[first : first + 4 * ROW_STEP : ROW_STEP, :]
+                nc.sync.dma_start(out=scale_tile[32 * q : 32 * q + 4, :].bitcast(I32), in_=rows.bitcast(I32))
+            return scale_tile
 
         xs = [place_scales(0)]
         x_win1 = sb.tile([P, T], I32, name="x_win1")
@@ -134,15 +136,16 @@ def tile_picked_zappnp_gelu_po_kernel(
                 entries = offs_sb[:, s0 // GROUP : s1 // GROUP]
                 nc.vector.tensor_copy(xg[g][:, s0:s1], win[:].bitcast(U32).indirect(entries))
 
-        w1_q = [quantize_w1_pass(w1_raw0, 0, (on_vector, on_vector))]
+        w1_q = [quantize_w1_pass(w1_raw0, 0, (on_vector, shared))]
         gather_words(0, x_win0, [0, S // 2, S])
         w1_q.append(quantize_w1_pass(w1_raw1, 1, (on_vector, shared)))
         gather_words(1, x_win1, [0, SLICE, 2 * SLICE, S])
 
-        h_groups = [(0, 2), (2, 4), (4, 6), (6, 7), (7, 8)]
+        last = CHUNKS - 1
+        h_groups = [(c, c + 2) for c in range(0, last - 1, 2)] + [(last - 1, last), (last, CHUNKS)]
         h_bf = {}
-        for c in range(S // CHUNK):
-            h_ps = bank(Y0_PARTS + c % (BANKS - Y0_PARTS), f"h_ps{c}")
+        for c in range(CHUNKS):
+            h_ps = bank(H_BANK0 + c % (BANKS - H_BANK0), f"h_ps{c}")
             cols = slice(CHUNK * c, CHUNK * (c + 1))
             for g in range(2):
                 for t in range(PACK):
@@ -154,12 +157,10 @@ def tile_picked_zappnp_gelu_po_kernel(
                         stop=(g == 1 and t == PACK - 1),
                         **stationary(w1_q[g], t),
                     )
-            c0, c1 = next_group = [group for group in h_groups if group[0] <= c < group[1]][0]
+            c0, c1 = [(first, end) for first, end in h_groups if first <= c < end][0]
             if c == c0:
-                h_bf[next_group] = sb.tile(
-                    [P, (c1 - c0) * CHUNK * PACK], BF16, name=f"h_bf{c0}", tag=f"h_bf{c0}", align_bytes=64
-                )
-            chunk_bf = h_bf[next_group][:, BANK * (c - c0) : BANK * (c - c0 + 1)]
+                h_bf[c0] = sb.tile([P, (c1 - c0) * BANK], BF16, name=f"h_bf{c0}", tag=f"h_bf{c0}", align_bytes=64)
+            chunk_bf = h_bf[c0][:, BANK * (c - c0) : BANK * (c - c0 + 1)]
             nc.scalar.activation(
                 chunk_bf.rearrange("p (n t) -> p n t", t=PACK), h_ps[:].rearrange("p (t n) -> p n t", t=PACK), GELU
             )
@@ -179,27 +180,29 @@ def tile_picked_zappnp_gelu_po_kernel(
                 **stationary(w2_q, t),
             )
 
-        last_chunk = S // CHUNK - 1
-        parts = [(0, 2), (2, 2 + PACK), (last_chunk, last_chunk + 1), (last_chunk - 1, last_chunk)]
-        for part, (c0, c1) in sorted(enumerate(parts), key=lambda entry: entry[1]):
-            acc = bank(part, f"y0_ps{part}")
+        last_bank = 2
+        parts = [(0, 0, 2), (1, 2, last - 1), (H_BANK0, last - 1, last), (last_bank, last, CHUNKS)]
+        for index, c0, c1 in parts:
+            acc = bank(index, f"y0_ps{index}")
             for g0, g1 in h_groups:
                 if c0 <= g0 < c1:
                     cols = slice(CHUNK * g0, CHUNK * g1)
                     nc.vector.quantize_mx(
-                        out=h_codes[:, cols].bitcast(FP8X4), scales=h_scales[:, cols], in_=h_bf[g0, g1][:]
+                        out=h_codes[:, cols].bitcast(FP8X4), scales=h_scales[:, cols], in_=h_bf[g0][:]
                     )
                     layer2(0, acc[:, CHUNK * (g0 - c0) : CHUNK * (g1 - c0)], cols)
-            if part == 0:
-                nc.vector.tensor_scalar_mul(y[0][:, CHUNK * c0 : CHUNK * c1], acc[:, 0 : CHUNK * (c1 - c0)], RESTART)
+            part_sb, part_ps = y[0][:, CHUNK * c0 : CHUNK * c1], acc[:, 0 : CHUNK * (c1 - c0)]
+            if c0 == 0:
+                nc.vector.tensor_scalar_mul(part_sb, part_ps, RESTART)
             else:
-                nc.scalar.activation(y[0][:, CHUNK * c0 : CHUNK * c1], acc[:, 0 : CHUNK * (c1 - c0)], COPY, scale=RESTART)
+                nc.scalar.activation(part_sb, part_ps, COPY, scale=RESTART)
 
-        w2_q.append(quantize(round_weight(on_vector, w2_raw, 1, "w2_bf1"), "w2_1", f"h_bf{last_chunk}"))
+        w2_q.append(quantize(round_weight(on_vector, w2_raw, 1, "w2_bf1"), "w2_1", f"h_bf{last}"))
+        y_banks = {1: (last_bank, 5), 2: (6, 7), 3: (0, 1)}
         for t in range(1, PACK):
             for half in range(2):
                 cols = slice(BANK * half, BANK * (half + 1))
-                acc = bank(2 if (t, half) == (1, 0) else (2 * t + 2 + half) % BANKS, f"y{t}_ps{half}")
+                acc = bank(y_banks[t][half], f"y{t}_ps{half}")
                 layer2(t, acc[:], cols)
                 nc.scalar.activation(y[t][:, cols], acc[:], COPY, scale=RESTART)
 

@@ -59,7 +59,7 @@ def tile_picked_zappnp_gelu_po_kernel(
             nc.sync.dma_start(out=tile[:, cols], in_=x_words[g].rearrange("p n r -> p (n r)").bitcast(I32)[:, cols])
 
         xs_win = sb.tile([P, T], U8, name="xs_win")
-        nc.gpsimd.memset(xs_win[:].bitcast(I32), 0)
+        nc.vector.memset(xs_win[:].bitcast(I32), 0)
         x_win0 = sb.tile([P, T], I32, name="x_win0")
         load_words(x_win0, 0, slice(0, 3 * T // 8))
         offs_sb = load_list(offs, "offs_sb")

@@ -27,7 +27,7 @@ GROUP = 16
 CHUNK = BANK // PACK
 CHUNKS = S // CHUNK
 SLICE = 2 * CHUNK
-H_BANK0 = 3
+H_BANK0 = 4
 SCALE_ROWS = 16
 ROW_STEP = P // (2 * SCALE_ROWS)
 RESTART = 0.2
@@ -88,11 +88,8 @@ def tile_picked_zappnp_gelu_po_kernel(
         xs.append(place_scales(1))
         w2_raw = load_weight(w2, "w2_raw")
         pos_sb = [load_list(pos1, "pos1_sb"), load_list(pos2, "pos2_sb")]
-        gate_row = []
-        for d in range(2):
-            row = sb.tile([P, V], F32, name=f"gate_row{d}", tag=f"gate_row{d}")
-            nc.sync.dma_start(out=row[:], in_=gate[d])
-            gate_row.append(row)
+        gate_row = sb.tile([P, 2, V], F32, name="gate_row")
+        nc.sync.dma_start(out=gate_row[:], in_=gate.rearrange("d p x -> p d x"))
         cen_sb = load_list(cen, "cen_sb")
         nxt_sb = [load_list(nxt1, "nxt1_sb"), load_list(nxt2, "nxt2_sb")]
         gate2_row = sb.tile([P, 2, U], F32, name="gate2_row")
@@ -139,11 +136,12 @@ def tile_picked_zappnp_gelu_po_kernel(
         w1_q = [quantize_w1_pass(w1_raw0, 0, (on_vector, shared))]
         gather_words(0, x_win0, [0, S // 2, S])
         w1_q.append(quantize_w1_pass(w1_raw1, 1, (on_vector, shared)))
-        gather_words(1, x_win1, [0, SLICE, 2 * SLICE, S])
+        gather_words(1, x_win1, [0, CHUNK, SLICE, 2 * SLICE, S])
 
         last = CHUNKS - 1
         h_groups = [(c, c + 2) for c in range(0, last - 1, 2)] + [(last - 1, last), (last, CHUNKS)]
         h_bf = {}
+        last_halves = [slice(0, CHUNK // 2), slice(CHUNK // 2, CHUNK)]
         for c in range(CHUNKS):
             h_ps = bank(H_BANK0 + c % (BANKS - H_BANK0), f"h_ps{c}")
             cols = slice(CHUNK * c, CHUNK * (c + 1))
@@ -160,10 +158,9 @@ def tile_picked_zappnp_gelu_po_kernel(
             c0, c1 = [(first, end) for first, end in h_groups if first <= c < end][0]
             if c == c0:
                 h_bf[c0] = sb.tile([P, (c1 - c0) * BANK], BF16, name=f"h_bf{c0}", tag=f"h_bf{c0}", align_bytes=64)
-            chunk_bf = h_bf[c0][:, BANK * (c - c0) : BANK * (c - c0 + 1)]
-            nc.scalar.activation(
-                chunk_bf.rearrange("p (n t) -> p n t", t=PACK), h_ps[:].rearrange("p (t n) -> p n t", t=PACK), GELU
-            )
+            chunk_bf = h_bf[c0][:, BANK * (c - c0) : BANK * (c - c0 + 1)].rearrange("p (n t) -> p n t", t=PACK)
+            for nodes in last_halves if c == last else [slice(0, CHUNK)]:
+                nc.scalar.activation(chunk_bf[:, nodes], h_ps[:].rearrange("p (t n) -> p n t", t=PACK)[:, nodes], GELU)
 
         w2_q = [quantize(round_weight(on_vector, w2_raw, 0, "w2_bf0"), "w2_0")]
         h_codes = sb.tile([P, S], U32, name="h_codes", align_bytes=64)
@@ -181,44 +178,51 @@ def tile_picked_zappnp_gelu_po_kernel(
             )
 
         last_bank = 2
-        parts = [(0, 0, 2), (1, 2, last - 1), (H_BANK0, last - 1, last), (last_bank, last, CHUNKS)]
+        parts = [(0, 0, 2), (1, 2, 4), (0, 4, last - 1), (3, last - 1, last), (last_bank, last, CHUNKS)]
         for index, c0, c1 in parts:
-            acc = bank(index, f"y0_ps{index}")
+            acc = bank(index, f"y0_ps{c0}")
             for g0, g1 in h_groups:
                 if c0 <= g0 < c1:
-                    cols = slice(CHUNK * g0, CHUNK * g1)
-                    nc.vector.quantize_mx(
-                        out=h_codes[:, cols].bitcast(FP8X4), scales=h_scales[:, cols], in_=h_bf[g0][:]
-                    )
-                    layer2(0, acc[:, CHUNK * (g0 - c0) : CHUNK * (g1 - c0)], cols)
+                    for nodes in last_halves if g0 == last else [slice(0, CHUNK * (g1 - g0))]:
+                        cols = slice(CHUNK * g0 + nodes.start, CHUNK * g0 + nodes.stop)
+                        nc.vector.quantize_mx(
+                            out=h_codes[:, cols].bitcast(FP8X4),
+                            scales=h_scales[:, cols],
+                            in_=h_bf[g0][:, PACK * nodes.start : PACK * nodes.stop],
+                        )
+                        layer2(0, acc[:, cols.start - CHUNK * c0 : cols.stop - CHUNK * c0], cols)
             part_sb, part_ps = y[0][:, CHUNK * c0 : CHUNK * c1], acc[:, 0 : CHUNK * (c1 - c0)]
-            if c0 == 0:
+            if c0 in (0, 2, last - 1):
                 nc.vector.tensor_scalar_mul(part_sb, part_ps, RESTART)
             else:
                 nc.scalar.activation(part_sb, part_ps, COPY, scale=RESTART)
 
         w2_q.append(quantize(round_weight(on_vector, w2_raw, 1, "w2_bf1"), "w2_1", f"h_bf{last}"))
-        y_banks = {1: (last_bank, 5), 2: (6, 7), 3: (0, 1)}
-        for t in range(1, PACK):
-            for half in range(2):
+        y_banks = {1: (6, 7), 2: (last_bank, 6), 3: (7, last_bank)}
+
+        def y_tile(t):
+            for half in (1, 0) if t == 2 else (0, 1):
                 cols = slice(BANK * half, BANK * (half + 1))
                 acc = bank(y_banks[t][half], f"y{t}_ps{half}")
                 layer2(t, acc[:], cols)
                 nc.scalar.activation(y[t][:, cols], acc[:], COPY, scale=RESTART)
+
 
         def gather_op(out, window, offsets, other, op):
             nc.vector.tensor_tensor(out, window[:].indirect(offsets), other, op)
 
         def gated_terms(terms, window, lists, gates):
             for d in range(2):
-                gather_op(terms[d], window, lists[d][:], gates[d], MULT)
+                gather_op(terms[d], window, lists[d][:], gates[:, d, :], MULT)
 
-        def add_on_tensor(terms, factor, banks, name):
+        def squares(width):
+            return [slice(col, col + P) for col in range(0, width, P)]
+
+        def turn_sum(terms, index, name, tag, factor=1.0):
             width = terms[0].shape[1]
-            squares = [slice(col, col + P) for col in range(0, width, P)]
-            sum_ps = bank(banks[0], name + "_sum_ps")
+            sum_ps = bank(index, name + "_sum_ps")
             for i, term in enumerate(terms):
-                for cols in squares:
+                for cols in squares(width):
                     nc.tensor.matmul(
                         sum_ps[:, cols],
                         lhsT=term[:, cols],
@@ -227,48 +231,57 @@ def tile_picked_zappnp_gelu_po_kernel(
                         stop=(i == len(terms) - 1 and cols.stop == width),
                         is_transpose=True,
                     )
-            turned = sb.tile([P, width], F32, name=name + "_turned", tag=name + "_turned", align_bytes=64)
-            nc.scalar.copy(out=turned[:], in_=sum_ps[:, 0:width])
-            back_ps = bank(banks[1], name + "_back_ps")
-            for cols in squares:
+            turned = sb.tile([P, width], F32, name=name + "_turned", tag=tag)
+            nc.scalar.activation(turned[:], sum_ps[:, 0:width], COPY, scale=factor)
+            return turned
+
+        def turn_back(turned, index, name):
+            width = turned.shape[1]
+            back_ps = bank(index, name + "_back_ps")
+            for cols in squares(width):
                 nc.tensor.transpose(back_ps[:, cols], turned[:, cols], ident[:])
-            total = sb.tile([P, width], F32, name=name + "_total")
-            nc.scalar.activation(total[:], back_ps[:, 0:width], COPY, scale=factor)
-            return total
+            return back_ps[:, 0:width]
 
-        z = []
-        for t in range(PACK):
-            near = sb.tile([P, 2, V], F32, name=f"near{t}")
-            terms = [near[:, d, :] for d in range(2)]
-            gated_terms(terms, y[t], pos_sb, [gate_row[d][:] for d in range(2)])
-            pair = (2, 3) if t % 2 == 0 else (4, 5)
-            total = add_on_tensor(terms, SPREAD / RESTART, pair if t < 2 else pair[::-1], f"near{t}")
-            z_t = sb.tile([P, V], F32, name=f"z{t}", tag="gate_row0" if t == 0 else f"z{t}")
-            gather_op(z_t[:], y[t], cen_sb[:], total[:], ADD)
-            z.append(z_t)
+        near, centre, z, turned, own = [], [], [], [], {}
+        near_banks = ((0, 4), (1, 5))
+        centre_tags = ("centre0", "centre1", "centre0", "turned0")
+        last_tile = PACK - 1
+        z_factor = SPREAD * SPREAD / RESTART
 
-        far0 = sb.tile([P, 2, U], F32, name="far0", tag="near2_turned", align_bytes=64)
-        far1_and_gates = sb.tile([P, 4, U], F32, name="far1_and_gates", tag="near3_turned", align_bytes=64)
-        far2 = sb.tile([P, 2, U], F32, name="far2", tag="far2")
-        far3 = sb.tile([P, 2, U], F32, name="far3")
-        nc.scalar.activation(far1_and_gates[:, 2:4, :], gate2_row[:], COPY, scale=SPREAD)
-        far_banks = ((5, 6), (7, 0), (1, 3))
-        far_total = []
-        for t, far in enumerate((far0, far1_and_gates, far2, far3)):
-            terms = [far[:, d, :] for d in range(2)]
-            scaled = t >= 2
-            gates = [far1_and_gates[:, 2 + d, :] if scaled else gate2_row[:, d, :] for d in range(2)]
-            gated_terms(terms, z[t], nxt_sb, gates)
-            if t < PACK - 1:
-                far_total.append(add_on_tensor(terms, 1.0 if scaled else SPREAD, far_banks[t], f"far{t}"))
-            else:
-                total = sb.tile([P, U], F32, name="far3_total")
-                nc.vector.tensor_tensor(total[:], terms[0], terms[1], ADD)
-                far_total.append(total)
+        def own_term(t, tag):
+            own[t] = sb.tile([P, U], F32, name=f"own{t}", tag=tag)
+            nc.scalar.activation(own[t][:], y[t][:].indirect(root_sb[:]), COPY)
 
-        res = [sb.tile([P, 2, U], F32, name="res0", tag="far2"), sb.tile([P, 2, U], F32, name="res1")]
+        def entries(offsets, cols):
+            return offsets[:, cols.start // GROUP : cols.stop // GROUP]
+
+        for step in range(PACK + 1):
+            if step + 1 < PACK:
+                y_tile(step + 1)
+            if step < PACK:
+                near.append(sb.tile([P, 2, V], F32, name=f"near{step}"))
+                gated_terms([near[step][:, d, :] for d in range(2)], y[step], pos_sb, gate_row)
+                centre.append(sb.tile([P, V], F32, name=f"centre{step}", tag=centre_tags[step]))
+                factor = SPREAD if step == last_tile else RESTART / SPREAD
+                nc.scalar.activation(centre[step][:], y[step][:].indirect(cen_sb[:]), COPY, scale=factor)
+            t = step - 1
+            if 0 <= t < last_tile:
+                terms = [near[t][:, 0, :], near[t][:, 1, :], centre[t][:]]
+                turned.append(turn_sum(terms, near_banks[t % 2][0], f"near{t}", f"turned{t}", z_factor))
+            if step == PACK:
+                own_term(0, "centre0")
+            t = step - 2
+            if 0 <= t < last_tile:
+                z.append(sb.tile([P, V], F32, name=f"z{t}"))
+                nc.scalar.copy(out=z[t][:], in_=turn_back(turned[t], near_banks[t % 2][1], f"near{t}"))
+        own_term(1, "turned2")
+        far = [[sb.tile([P, U], F32, name=f"far{t}{d}", tag=f"far{t}{d}") for d in range(2)] for t in range(last_tile)]
+        res = [sb.tile([P, 2, U], F32, name=f"res{u}") for u in range(2)]
         out_rows = out_0.rearrange("(p t) x -> p t x", t=PACK)
-        res_bf = sb.tile([P, U * PACK], BF16, name="res_bf", tag="far2_turned", align_bytes=64)
+        res_bf = sb.tile([P, U * PACK], BF16, name="res_bf", align_bytes=64)
+        o_codes = sb.tile([P, U], U32, name="o_codes", align_bytes=64)
+        o_scales = sb.tile([P, U], U8, name="o_scales", align_bytes=64)
+        col_halves = [slice(0, U // 2), slice(U // 2, U)]
 
         def round_result(engine_copy, u, cols):
             engine_copy(
@@ -276,18 +289,41 @@ def tile_picked_zappnp_gelu_po_kernel(
                 in_=res[u][:, :, cols].rearrange("p t x -> p x t"),
             )
 
-        for t in (0, 1, 3):
-            gather_op(res[t // 2][:, t % 2, :], y[t], root_sb[:], far_total[t][:], ADD)
-            nc.sync.dma_start(out=out_rows[:, t, :], in_=res[t // 2][:, t % 2, :])
-            if t == 1:
-                round_result(nc.scalar.copy, 0, slice(0, U))
-        col_halves = [slice(0, U // 2), slice(U // 2, U)]
+        near_total = sb.tile([P, V], F32, name="near_total", tag="turned1")
+        nc.vector.tensor_tensor(near_total[:], near[3][:, 0, :], near[3][:, 1, :], ADD)
+        for t in range(2):
+            gated_terms([term[:] for term in far[t]], z[t], nxt_sb, gate2_row)
+        plain2 = sb.tile([P, U], F32, name="plain2")
+        nc.scalar.activation(plain2[:], z[2][:].indirect(nxt_sb[0][:]), COPY)
+        far_banks = ((0, 7), (1, 6))
+        far_turned = []
+        for t in range(2):
+            terms = [far[t][0][:], far[t][1][:], own[t][:]]
+            far_turned.append(turn_sum(terms, far_banks[t][0], f"far{t}", f"far_turned{t}"))
+            own_term(last_tile - t, ("centre0", "turned2")[t])
+        z.append(sb.tile([P, V], F32, name="z3", tag="far00"))
+        nc.vector.scalar_tensor_tensor(
+            out=z[3][:], in0=near_total[:], scalar=z_factor, in1=centre[3][:], op0=MULT, op1=ADD
+        )
+        for t in range(2):
+            nc.scalar.copy(out=res[0][:, t, :], in_=turn_back(far_turned[t], far_banks[t][1], f"far{t}"))
+        nc.sync.dma_start(out=out_rows[:, 0:2, :], in_=res[0][:])
+        round_result(nc.scalar.copy, 0, slice(0, U))
+
+        far3 = sb.tile([P, 2, U], F32, name="far3", tag="far11")
+        total = [sb.tile([P, U], F32, name=f"far_total{t}") for t in (2, 3)]
+        gather_op(far[2][1][:], z[2], nxt_sb[1][:], gate2_row[:, 1, :], MULT)
+        gather_op(far3[:, 0, :], z[3], nxt_sb[0][:], gate2_row[:, 0, :], MULT)
+        nc.vector.tensor_tensor(far[2][0][:], plain2[:], gate2_row[:, 0, :], MULT)
         for cols in col_halves:
-            entries = root_sb[:, cols.start // GROUP : cols.stop // GROUP]
-            gather_op(res[1][:, 0, cols], y[2], entries, far_total[2][:, cols], ADD)
-        nc.sync.dma_start(out=out_rows[:, 2, :], in_=res[1][:, 0, :])
-        o_codes = sb.tile([P, U], U32, name="o_codes", align_bytes=64)
-        o_scales = sb.tile([P, U], U8, name="o_scales", align_bytes=64)
+            gather_op(far3[:, 1, cols], z[3], entries(nxt_sb[1], cols), gate2_row[:, 1, cols], MULT)
+            if cols.start == 0:
+                nc.vector.tensor_tensor(total[0][:], far[2][0][:], far[2][1][:], ADD)
+                nc.vector.tensor_tensor(total[1][:], far3[:, 0, :], own[3][:], ADD)
+        nc.vector.tensor_tensor(res[1][:, 0, :], total[0][:], own[2][:], ADD)
+        for cols in col_halves:
+            nc.vector.tensor_tensor(res[1][:, 1, cols], total[1][:, cols], far3[:, 1, cols], ADD)
+        nc.sync.dma_start(out=out_rows[:, 2:PACK, :], in_=res[1][:])
         for cols in col_halves:
             round_result(nc.vector.tensor_copy, 1, cols)
         for cols in col_halves:

@@ -59,33 +59,34 @@ def tile_picked_zappnp_gelu_po_kernel(
             nc.sync.dma_start(out=tile[:, cols], in_=x_words[g].rearrange("p n r -> p (n r)").bitcast(I32)[:, cols])
 
         xs_win = sb.tile([P, T], U8, name="xs_win")
-        nc.vector.memset(xs_win[:].bitcast(I32), 0)
+        nc.gpsimd.memset(xs_win[:].bitcast(I32), 0)
         x_win0 = sb.tile([P, T], I32, name="x_win0")
         load_words(x_win0, 0, slice(0, 3 * T // 8))
         offs_sb = load_list(offs, "offs_sb")
-        nc.sync.dma_start(
-            out=xs_win[0:P:ROW_STEP, :].bitcast(I32), in_=x_scales.rearrange("g r c -> (g r) c").bitcast(I32)
-        )
+        nc.sync.dma_start(out=xs_win[ROW_STEP : P : 2 * ROW_STEP, :].bitcast(I32), in_=x_scales[0].bitcast(I32))
+        for q in range(4):
+            nc.sync.dma_start(
+                out=xs_win[32 * q : 32 * q + 4, :].bitcast(I32), in_=x_scales[1, 4 * q : 4 * q + 4, :].bitcast(I32)
+            )
         w1_raw0 = load_weight(w1[0:K_PASS, :], "w1_raw0")
         load_words(x_win0, 0, slice(3 * T // 8, T))
         w1_raw1 = load_weight(w1[K_PASS:K, :], "w1_raw1")
 
-        xs_picked = sb.tile([P, S], U8, name="xs_picked")
+        xs_picked = sb.tile([P, S], U8, name="xs_picked", align_bytes=64)
         nc.vector.tensor_copy(xs_picked[:], xs_win[:].indirect(offs_sb[:]))
 
         def place_scales(g):
             scale_tile = sb.tile([P, S], U8, name=f"xs{g}", align_bytes=64)
             nc.vector.memset(scale_tile[:].bitcast(I32), 0)
             for q in range(4):
-                first = ROW_STEP * (SCALE_ROWS * g + 4 * q)
-                rows = xs_picked[first : first + 4 * ROW_STEP : ROW_STEP, :]
+                rows = xs_picked[32 * q + ROW_STEP : 32 * (q + 1) : 2 * ROW_STEP, :]
                 nc.sync.dma_start(out=scale_tile[32 * q : 32 * q + 4, :].bitcast(I32), in_=rows.bitcast(I32))
             return scale_tile
 
         xs = [place_scales(0)]
         x_win1 = sb.tile([P, T], I32, name="x_win1")
         load_words(x_win1, 1, slice(0, T))
-        xs.append(place_scales(1))
+        xs.append(xs_picked)
         w2_raw = load_weight(w2, "w2_raw")
         pos_sb = [load_list(pos1, "pos1_sb"), load_list(pos2, "pos2_sb")]
         gate_row = sb.tile([P, 2, V], F32, name="gate_row")
@@ -308,7 +309,8 @@ def tile_picked_zappnp_gelu_po_kernel(
         for t in range(2):
             nc.scalar.copy(out=res[0][:, t, :], in_=turn_back(far_turned[t], far_banks[t][1], f"far{t}"))
         nc.sync.dma_start(out=out_rows[:, 0:2, :], in_=res[0][:])
-        round_result(nc.scalar.copy, 0, slice(0, U))
+        for cols in col_halves:
+            round_result(nc.scalar.copy, 0, cols)
 
         far3 = sb.tile([P, 2, U], F32, name="far3", tag="far11")
         total = [sb.tile([P, U], F32, name=f"far_total{t}") for t in (2, 3)]

@@ -27,7 +27,7 @@ GROUP = 16
 CHUNK = BANK // PACK
 CHUNKS = S // CHUNK
 SLICE = 2 * CHUNK
-H_BANK0 = 4
+H_BANK0 = 3
 SCALE_ROWS = 16
 ROW_STEP = P // (2 * SCALE_ROWS)
 RESTART = 0.2
@@ -63,10 +63,10 @@ def tile_picked_zappnp_gelu_po_kernel(
         x_win0 = sb.tile([P, T], I32, name="x_win0")
         load_words(x_win0, 0, slice(0, 3 * T // 8))
         offs_sb = load_list(offs, "offs_sb")
-        nc.sync.dma_start(out=xs_win[ROW_STEP : P : 2 * ROW_STEP, :].bitcast(I32), in_=x_scales[0].bitcast(I32))
+        nc.sync.dma_start(out=xs_win[ROW_STEP : P : 2 * ROW_STEP, :].bitcast(I32), in_=x_scales[1].bitcast(I32))
         for q in range(4):
             nc.sync.dma_start(
-                out=xs_win[32 * q : 32 * q + 4, :].bitcast(I32), in_=x_scales[1, 4 * q : 4 * q + 4, :].bitcast(I32)
+                out=xs_win[32 * q : 32 * q + 4, :].bitcast(I32), in_=x_scales[0, 4 * q : 4 * q + 4, :].bitcast(I32)
             )
         w1_raw0 = load_weight(w1[0:K_PASS, :], "w1_raw0")
         load_words(x_win0, 0, slice(3 * T // 8, T))
@@ -83,10 +83,9 @@ def tile_picked_zappnp_gelu_po_kernel(
                 nc.sync.dma_start(out=scale_tile[32 * q : 32 * q + 4, :].bitcast(I32), in_=rows.bitcast(I32))
             return scale_tile
 
-        xs = [place_scales(0)]
+        xs = [xs_picked, place_scales(1)]
         x_win1 = sb.tile([P, T], I32, name="x_win1")
         load_words(x_win1, 1, slice(0, T))
-        xs.append(xs_picked)
         w2_raw = load_weight(w2, "w2_raw")
         pos_sb = [load_list(pos1, "pos1_sb"), load_list(pos2, "pos2_sb")]
         gate_row = sb.tile([P, 2, V], F32, name="gate_row")
@@ -199,7 +198,7 @@ def tile_picked_zappnp_gelu_po_kernel(
                 nc.scalar.activation(part_sb, part_ps, COPY, scale=RESTART)
 
         w2_q.append(quantize(round_weight(on_vector, w2_raw, 1, "w2_bf1"), "w2_1", f"h_bf{last}"))
-        y_banks = {1: (6, 7), 2: (last_bank, 6), 3: (7, last_bank)}
+        y_banks = {1: (4, 5), 2: (last_bank, 4), 3: (5, last_bank)}
 
         def y_tile(t):
             for half in (1, 0) if t == 2 else (0, 1):
@@ -244,7 +243,7 @@ def tile_picked_zappnp_gelu_po_kernel(
             return back_ps[:, 0:width]
 
         near, centre, z, turned, own = [], [], [], [], {}
-        near_banks = ((0, 4), (1, 5))
+        near_banks = ((0, 6), (1, 7))
         centre_tags = ("centre0", "centre1", "centre0", "turned0")
         last_tile = PACK - 1
         z_factor = SPREAD * SPREAD / RESTART
@@ -296,7 +295,7 @@ def tile_picked_zappnp_gelu_po_kernel(
             gated_terms([term[:] for term in far[t]], z[t], nxt_sb, gate2_row)
         plain2 = sb.tile([P, U], F32, name="plain2")
         nc.scalar.activation(plain2[:], z[2][:].indirect(nxt_sb[0][:]), COPY)
-        far_banks = ((0, 7), (1, 6))
+        far_banks = ((0, 5), (1, 4))
         far_turned = []
         for t in range(2):
             terms = [far[t][0][:], far[t][1][:], own[t][:]]

@@ -64,10 +64,8 @@ def tile_picked_zappnp_gelu_po_kernel(
         load_words(x_win0, 0, slice(0, 3 * T // 8))
         offs_sb = load_list(offs, "offs_sb")
         nc.sync.dma_start(out=xs_win[ROW_STEP : P : 2 * ROW_STEP, :].bitcast(I32), in_=x_scales[1].bitcast(I32))
-        for q in range(4):
-            nc.sync.dma_start(
-                out=xs_win[32 * q : 32 * q + 4, :].bitcast(I32), in_=x_scales[0, 4 * q : 4 * q + 4, :].bitcast(I32)
-            )
+        for r in range(4):
+            nc.sync.dma_start(out=xs_win[r:P:32, :].bitcast(I32), in_=x_scales[0, r:SCALE_ROWS:4, :].bitcast(I32))
         w1_raw0 = load_weight(w1[0:K_PASS, :], "w1_raw0")
         load_words(x_win0, 0, slice(3 * T // 8, T))
         w1_raw1 = load_weight(w1[K_PASS:K, :], "w1_raw1")
@@ -78,9 +76,9 @@ def tile_picked_zappnp_gelu_po_kernel(
         def place_scales(g):
             scale_tile = sb.tile([P, S], U8, name=f"xs{g}", align_bytes=64)
             nc.vector.memset(scale_tile[:].bitcast(I32), 0)
-            for q in range(4):
-                rows = xs_picked[32 * q + ROW_STEP : 32 * (q + 1) : 2 * ROW_STEP, :]
-                nc.sync.dma_start(out=scale_tile[32 * q : 32 * q + 4, :].bitcast(I32), in_=rows.bitcast(I32))
+            for r in range(4):
+                rows = xs_picked[ROW_STEP * (2 * r + 1) : P : 32, :]
+                nc.sync.dma_start(out=scale_tile[r:P:32, :].bitcast(I32), in_=rows.bitcast(I32))
             return scale_tile
 
         xs = [xs_picked, place_scales(1)]

@@ -27,7 +27,7 @@ GROUP = 16
 CHUNK = BANK // PACK
 CHUNKS = S // CHUNK
 SLICE = 2 * CHUNK
-H_BANK0 = 3
+H_BANKS = (5, 6, 7, 1, 2, 3, 4, 5)
 SCALE_ROWS = 16
 ROW_STEP = P // (2 * SCALE_ROWS)
 RESTART = 0.2
@@ -141,7 +141,7 @@ def tile_picked_zappnp_gelu_po_kernel(
         h_bf = {}
         last_halves = [slice(0, CHUNK // 2), slice(CHUNK // 2, CHUNK)]
         for c in range(CHUNKS):
-            h_ps = bank(H_BANK0 + c % (BANKS - H_BANK0), f"h_ps{c}")
+            h_ps = bank(H_BANKS[c], f"h_ps{c}")
             cols = slice(CHUNK * c, CHUNK * (c + 1))
             for g in range(2):
                 for t in range(PACK):
@@ -176,7 +176,7 @@ def tile_picked_zappnp_gelu_po_kernel(
             )
 
         last_bank = 2
-        parts = [(0, 0, 2), (1, 2, 4), (0, 4, last - 1), (3, last - 1, last), (last_bank, last, CHUNKS)]
+        parts = [(0, 0, 2), (6, 2, 4), (0, 4, last - 1), (3, last - 1, last), (last_bank, last, CHUNKS)]
         for index, c0, c1 in parts:
             acc = bank(index, f"y0_ps{c0}")
             for g0, g1 in h_groups:

from contextlib import ExitStack

import concourse.mybir as mybir
from concourse.masks import make_identity

K, T, S, V, H, N, U = 1024, 2048, 1024, 512, 512, 512, 256
FLOPS = 2 * K * H * S + 2 * H * N * S

F32 = mybir.dt.float32
BF16 = mybir.dt.bfloat16
I32 = mybir.dt.int32
U32 = mybir.dt.uint32
U16 = mybir.dt.uint16
U8 = mybir.dt.uint8
FP8X4 = mybir.dt.float8_e4m3fn_x4
GELU = mybir.ActivationFunctionType.Gelu_apprx_tanh
COPY = mybir.ActivationFunctionType.Copy
MULT = mybir.AluOpType.mult
ADD = mybir.AluOpType.add

P = 128
PACK = 4
K_PASS = P * PACK
BANK = 512
BANKS = 8
GROUP = 16
CHUNK = BANK // PACK
CHUNKS = S // CHUNK
SLICE = 2 * CHUNK
H_BANKS = (5, 6, 7, 1, 2, 3, 4, 5)
SCALE_ROWS = 16
ROW_STEP = P // (2 * SCALE_ROWS)
RESTART = 0.2
SPREAD = 0.8


def tile_picked_zappnp_gelu_po_kernel(
    tc, x_words, x_scales, w1, w2, gate, gate2, offs, cen, pos1, pos2, nxt1, nxt2, root, out_0, out_1, out_2
):
    nc = tc.nc
    with ExitStack() as ctx:
        sb = ctx.enter_context(tc.tile_pool(name="sb", bufs=1))
        psum = ctx.enter_context(tc.psum_pool(name="psum", bufs=1))

        def bank(index, name):
            return psum.tile([P, BANK], F32, name=name, tag=f"bank{index}")

        def load_list(src, name):
            tile = sb.tile(list(src.shape), U16, name=name)
            nc.sync.dma_start(tile[:], src)
            return tile

        def load_weight(rows, name):
            raw = sb.tile([P, PACK, rows.shape[1]], F32, name=name)
            nc.sync.dma_start(out=raw[:], in_=rows.rearrange("(p j) c -> p j c", j=PACK))
            return raw

        def load_words(tile, g, cols):
            nc.sync.dma_start(out=tile[:, cols], in_=x_words[g].rearrange("p n r -> p (n r)").bitcast(I32)[:, cols])

        xs_win = sb.tile([P, T], U8, name="xs_win")
        nc.gpsimd.memset(xs_win[:].bitcast(I32), 0)
        x_win0 = sb.tile([P, T], I32, name="x_win0")
        load_words(x_win0, 0, slice(0, 3 * T // 8))
        offs_sb = load_list(offs, "offs_sb")
        nc.sync.dma_start(out=xs_win[ROW_STEP : P : 2 * ROW_STEP, :].bitcast(I32), in_=x_scales[1].bitcast(I32))
        for r in range(4):
            nc.sync.dma_start(out=xs_win[r:P:32, :].bitcast(I32), in_=x_scales[0, r:SCALE_ROWS:4, :].bitcast(I32))
        w1_raw0 = load_weight(w1[0:K_PASS, :], "w1_raw0")
        load_words(x_win0, 0, slice(3 * T // 8, T))
        w1_raw1 = load_weight(w1[K_PASS:K, :], "w1_raw1")

        xs_picked = sb.tile([P, S], U8, name="xs_picked", align_bytes=64)
        nc.vector.tensor_copy(xs_picked[:], xs_win[:].indirect(offs_sb[:]))

        def place_scales(g):
            scale_tile = sb.tile([P, S], U8, name=f"xs{g}", align_bytes=64)
            nc.vector.memset(scale_tile[:].bitcast(I32), 0)
            for r in range(4):
                rows = xs_picked[ROW_STEP * (2 * r + 1) : P : 32, :]
                nc.sync.dma_start(out=scale_tile[r:P:32, :].bitcast(I32), in_=rows.bitcast(I32))
            return scale_tile

        xs = [xs_picked, place_scales(1)]
        x_win1 = sb.tile([P, T], I32, name="x_win1")
        load_words(x_win1, 1, slice(0, T))
        w2_raw = load_weight(w2, "w2_raw")
        pos_sb = [load_list(pos1, "pos1_sb"), load_list(pos2, "pos2_sb")]
        gate_row = sb.tile([P, 2, V], F32, name="gate_row")
        nc.sync.dma_start(out=gate_row[:], in_=gate.rearrange("d p x -> p d x"))
        cen_sb = load_list(cen, "cen_sb")
        nxt_sb = [load_list(nxt1, "nxt1_sb"), load_list(nxt2, "nxt2_sb")]
        gate2_row = sb.tile([P, 2, U], F32, name="gate2_row")
        nc.sync.dma_start(out=gate2_row[:], in_=gate2.rearrange("d p x -> p d x"))
        root_sb = load_list(root, "root_sb")

        ident = sb.tile([P, P], F32, name="ident")
        make_identity(nc, ident[:])

        def round_weight(shares, raw, u, name):
            grouped = sb.tile([P, 2 * P * PACK], BF16, name=name, align_bytes=64)
            src = raw[:].rearrange("p j (m t) -> p m j t", t=PACK)[:, :, :, 2 * u : 2 * u + 2]
            dst = grouped[:].rearrange("p (t m j) -> p m j t", t=2, j=PACK)
            for engine_copy, cols in shares:
                engine_copy(out=dst[:, cols], in_=src[:, cols])
            return grouped

        def quantize(grouped, name, tag=None):
            width = grouped.shape[1] // PACK
            codes = sb.tile([P, width], U32, name=name + "_codes", tag=tag or name + "_codes", align_bytes=64)
            scales = sb.tile([P, width], U8, name=name + "_scales", align_bytes=64)
            nc.vector.quantize_mx(out=codes[:].bitcast(FP8X4), scales=scales[:], in_=grouped[:])
            return codes, scales

        def stationary(pairs, t):
            codes, scales = pairs[t // 2]
            cols = slice(P * (t % 2), P * (t % 2 + 1))
            return dict(lhsT=codes[:, cols].bitcast(FP8X4), lhsT_scale=scales[:, cols])

        on_vector = [(nc.vector.tensor_copy, slice(0, P))]
        shared = [(nc.vector.tensor_copy, slice(0, P // 4)), (nc.scalar.copy, slice(P // 4, P))]

        def quantize_w1_pass(raw, g, shares):
            halves = [round_weight(shares[u], raw, u, f"w1_bf{g}{u}") for u in range(2)]
            return [quantize(half, f"w1_{g}{u}") for u, half in enumerate(halves)]

        xg = [sb.tile([P, S], U32, name=f"xg{g}", align_bytes=64) for g in range(2)]

        def gather_words(g, win, cuts):
            for s0, s1 in zip(cuts, cuts[1:]):
                entries = offs_sb[:, s0 // GROUP : s1 // GROUP]
                nc.vector.tensor_copy(xg[g][:, s0:s1], win[:].bitcast(U32).indirect(entries))

        w1_q = [quantize_w1_pass(w1_raw0, 0, (on_vector, shared))]
        gather_words(0, x_win0, [0, S // 2, S])
        w1_q.append(quantize_w1_pass(w1_raw1, 1, (on_vector, shared)))
        gather_words(1, x_win1, [0, CHUNK, SLICE, 2 * SLICE, S])

        last = CHUNKS - 1
        h_groups = [(c, c + 2) for c in range(0, last - 1, 2)] + [(last - 1, last), (last, CHUNKS)]
        h_bf = {}
        last_halves = [slice(0, CHUNK // 2), slice(CHUNK // 2, CHUNK)]
        for c in range(CHUNKS):
            h_ps = bank(H_BANKS[c], f"h_ps{c}")
            cols = slice(CHUNK * c, CHUNK * (c + 1))
            for g in range(2):
                for t in range(PACK):
                    nc.tensor.matmul_mx(
                        out=h_ps[:, CHUNK * t : CHUNK * (t + 1)],
                        rhs=xg[g][:, cols].bitcast(FP8X4),
                        rhs_scale=xs[g][:, cols],
                        start=(g == 0 and t == 0),
                        stop=(g == 1 and t == PACK - 1),
                        **stationary(w1_q[g], t),
                    )
            c0, c1 = [(first, end) for first, end in h_groups if first <= c < end][0]
            if c == c0:
                h_bf[c0] = sb.tile([P, (c1 - c0) * BANK], BF16, name=f"h_bf{c0}", tag=f"h_bf{c0}", align_bytes=64)
            chunk_bf = h_bf[c0][:, BANK * (c - c0) : BANK * (c - c0 + 1)].rearrange("p (n t) -> p n t", t=PACK)
            for nodes in last_halves if c == last else [slice(0, CHUNK)]:
                nc.scalar.activation(chunk_bf[:, nodes], h_ps[:].rearrange("p (t n) -> p n t", t=PACK)[:, nodes], GELU)

        w2_q = [quantize(round_weight(on_vector, w2_raw, 0, "w2_bf0"), "w2_0")]
        h_codes = sb.tile([P, S], U32, name="h_codes", align_bytes=64)
        h_scales = sb.tile([P, S], U8, name="h_scales", align_bytes=64)
        y = [sb.tile([P, S], F32, name=f"y{t}") for t in range(PACK)]

        def layer2(t, acc, cols):
            nc.tensor.matmul_mx(
                out=acc,
                rhs=h_codes[:, cols].bitcast(FP8X4),
                rhs_scale=h_scales[:, cols],
                start=True,
                stop=True,
                **stationary(w2_q, t),
            )

        last_bank = 2
        parts = [(0, 0, 2), (6, 2, 4), (0, 4, last - 1), (3, last - 1, last), (last_bank, last, CHUNKS)]
        for index, c0, c1 in parts:
            acc = bank(index, f"y0_ps{c0}")
            for g0, g1 in h_groups:
                if c0 <= g0 < c1:
                    for nodes in last_halves if g0 == last else [slice(0, CHUNK * (g1 - g0))]:
                        cols = slice(CHUNK * g0 + nodes.start, CHUNK * g0 + nodes.stop)
                        nc.vector.quantize_mx(
                            out=h_codes[:, cols].bitcast(FP8X4),
                            scales=h_scales[:, cols],
                            in_=h_bf[g0][:, PACK * nodes.start : PACK * nodes.stop],
                        )
                        layer2(0, acc[:, cols.start - CHUNK * c0 : cols.stop - CHUNK * c0], cols)
            part_sb, part_ps = y[0][:, CHUNK * c0 : CHUNK * c1], acc[:, 0 : CHUNK * (c1 - c0)]
            if c0 in (0, 2, last - 1):
                nc.vector.tensor_scalar_mul(part_sb, part_ps, RESTART)
            else:
                nc.scalar.activation(part_sb, part_ps, COPY, scale=RESTART)

        w2_q.append(quantize(round_weight(on_vector, w2_raw, 1, "w2_bf1"), "w2_1", f"h_bf{last}"))
        y_banks = {1: (4, 5), 2: (last_bank, 4), 3: (5, last_bank)}

        def y_tile(t):
            for half in (1, 0) if t == 2 else (0, 1):
                cols = slice(BANK * half, BANK * (half + 1))
                acc = bank(y_banks[t][half], f"y{t}_ps{half}")
                layer2(t, acc[:], cols)
                nc.scalar.activation(y[t][:, cols], acc[:], COPY, scale=RESTART)


        def gather_op(out, window, offsets, other, op):
            nc.vector.tensor_tensor(out, window[:].indirect(offsets), other, op)

        def gated_terms(terms, window, lists, gates):
            for d in range(2):
                gather_op(terms[d], window, lists[d][:], gates[:, d, :], MULT)

        def squares(width):
            return [slice(col, col + P) for col in range(0, width, P)]

        def turn_sum(terms, index, name, tag, factor=1.0):
            width = terms[0].shape[1]
            sum_ps = bank(index, name + "_sum_ps")
            for i, term in enumerate(terms):
                for cols in squares(width):
                    nc.tensor.matmul(
                        sum_ps[:, cols],
                        lhsT=term[:, cols],
                        rhs=ident[:],
                        start=(i == 0 and cols.start == 0),
                        stop=(i == len(terms) - 1 and cols.stop == width),
                        is_transpose=True,
                    )
            turned = sb.tile([P, width], F32, name=name + "_turned", tag=tag)
            nc.scalar.activation(turned[:], sum_ps[:, 0:width], COPY, scale=factor)
            return turned

        def turn_back(turned, index, name):
            width = turned.shape[1]
            back_ps = bank(index, name + "_back_ps")
            for cols in squares(width):
                nc.tensor.transpose(back_ps[:, cols], turned[:, cols], ident[:])
            return back_ps[:, 0:width]

        near, centre, z, turned, own = [], [], [], [], {}
        near_banks = ((0, 6), (1, 7))
        centre_tags = ("centre0", "centre1", "centre0", "turned0")
        last_tile = PACK - 1
        z_factor = SPREAD * SPREAD / RESTART

        def own_term(t, tag):
            own[t] = sb.tile([P, U], F32, name=f"own{t}", tag=tag)
            nc.scalar.activation(own[t][:], y[t][:].indirect(root_sb[:]), COPY)

        def entries(offsets, cols):
            return offsets[:, cols.start // GROUP : cols.stop // GROUP]

        for step in range(PACK + 1):
            if step + 1 < PACK:
                y_tile(step + 1)
            if step < PACK:
                near.append(sb.tile([P, 2, V], F32, name=f"near{step}"))
                gated_terms([near[step][:, d, :] for d in range(2)], y[step], pos_sb, gate_row)
                centre.append(sb.tile([P, V], F32, name=f"centre{step}", tag=centre_tags[step]))
                factor = SPREAD if step == last_tile else RESTART / SPREAD
                nc.scalar.activation(centre[step][:], y[step][:].indirect(cen_sb[:]), COPY, scale=factor)
            t = step - 1
            if 0 <= t < last_tile:
                terms = [near[t][:, 0, :], near[t][:, 1, :], centre[t][:]]
                turned.append(turn_sum(terms, near_banks[t % 2][0], f"near{t}", f"turned{t}", z_factor))
            if step == PACK:
                own_term(0, "centre0")
            t = step - 2
            if 0 <= t < last_tile:
                z.append(sb.tile([P, V], F32, name=f"z{t}"))
                nc.scalar.copy(out=z[t][:], in_=turn_back(turned[t], near_banks[t % 2][1], f"near{t}"))
        own_term(1, "turned2")
        far = [[sb.tile([P, U], F32, name=f"far{t}{d}", tag=f"far{t}{d}") for d in range(2)] for t in range(last_tile)]
        res = [sb.tile([P, 2, U], F32, name=f"res{u}") for u in range(2)]
        out_rows = out_0.rearrange("(p t) x -> p t x", t=PACK)
        res_bf = sb.tile([P, U * PACK], BF16, name="res_bf", align_bytes=64)
        o_codes = sb.tile([P, U], U32, name="o_codes", align_bytes=64)
        o_scales = sb.tile([P, U], U8, name="o_scales", align_bytes=64)
        col_halves = [slice(0, U // 2), slice(U // 2, U)]

        def round_result(engine_copy, u, cols):
            engine_copy(
                out=res_bf[:].rearrange("p (x t) -> p x t", t=PACK)[:, cols, 2 * u : 2 * u + 2],
                in_=res[u][:, :, cols].rearrange("p t x -> p x t"),
            )

        near_total = sb.tile([P, V], F32, name="near_total", tag="turned1")
        nc.vector.tensor_tensor(near_total[:], near[3][:, 0, :], near[3][:, 1, :], ADD)
        for t in range(2):
            gated_terms([term[:] for term in far[t]], z[t], nxt_sb, gate2_row)
        plain2 = sb.tile([P, U], F32, name="plain2")
        nc.scalar.activation(plain2[:], z[2][:].indirect(nxt_sb[0][:]), COPY)
        far_banks = ((0, 5), (1, 4))
        far_turned = []
        for t in range(2):
            terms = [far[t][0][:], far[t][1][:], own[t][:]]
            far_turned.append(turn_sum(terms, far_banks[t][0], f"far{t}", f"far_turned{t}"))
            own_term(last_tile - t, ("centre0", "turned2")[t])
        z.append(sb.tile([P, V], F32, name="z3", tag="far00"))
        nc.vector.scalar_tensor_tensor(
            out=z[3][:], in0=near_total[:], scalar=z_factor, in1=centre[3][:], op0=MULT, op1=ADD
        )
        for t in range(2):
            nc.scalar.copy(out=res[0][:, t, :], in_=turn_back(far_turned[t], far_banks[t][1], f"far{t}"))
        nc.sync.dma_start(out=out_rows[:, 0:2, :], in_=res[0][:])
        for cols in col_halves:
            round_result(nc.scalar.copy, 0, cols)

        far3 = sb.tile([P, 2, U], F32, name="far3", tag="far11")
        total = [sb.tile([P, U], F32, name=f"far_total{t}") for t in (2, 3)]
        gather_op(far[2][1][:], z[2], nxt_sb[1][:], gate2_row[:, 1, :], MULT)
        gather_op(far3[:, 0, :], z[3], nxt_sb[0][:], gate2_row[:, 0, :], MULT)
        nc.vector.tensor_tensor(far[2][0][:], plain2[:], gate2_row[:, 0, :], MULT)
        for cols in col_halves:
            gather_op(far3[:, 1, cols], z[3], entries(nxt_sb[1], cols), gate2_row[:, 1, cols], MULT)
            if cols.start == 0:
                nc.vector.tensor_tensor(total[0][:], far[2][0][:], far[2][1][:], ADD)
                nc.vector.tensor_tensor(total[1][:], far3[:, 0, :], own[3][:], ADD)
        nc.vector.tensor_tensor(res[1][:, 0, :], total[0][:], own[2][:], ADD)
        for cols in col_halves:
            nc.vector.tensor_tensor(res[1][:, 1, cols], total[1][:, cols], far3[:, 1, cols], ADD)
        nc.sync.dma_start(out=out_rows[:, 2:PACK, :], in_=res[1][:])
        for cols in col_halves:
            round_result(nc.vector.tensor_copy, 1, cols)
        for cols in col_halves:
            nc.vector.quantize_mx(
                out=o_codes[:, cols].bitcast(FP8X4),
                scales=o_scales[:, cols],
                in_=res_bf[:, PACK * cols.start : PACK * cols.stop],
            )

        nc.sync.dma_start(out=out_1[0].rearrange("p n r -> p (n r)").bitcast(I32), in_=o_codes[:].bitcast(I32))
        for q in range(4):
            queue = nc.scalar if q % 2 == 0 else nc.sync
            queue.dma_start(
                out=out_2[0, 4 * q : 4 * q + 4, :].bitcast(I32), in_=o_scales[32 * q : 32 * q + 4, :].bitcast(I32)
            )
